import numpy as np
import ml_dtypes


def mxq(x, axis, fmt="e4m3"):
    dtype, down = {"e4m3": (ml_dtypes.float8_e4m3fn, 7), "e5m2": (ml_dtypes.float8_e5m2, 14)}[fmt]
    v = np.moveaxis(np.asarray(x, np.float32).astype(ml_dtypes.bfloat16).astype(np.float64), axis, -1)
    blocks = v.reshape(v.shape[:-1] + (-1, 32))
    amax = np.abs(blocks).max(-1, keepdims=True)
    byte = np.maximum(np.where(amax > 0, np.frexp(amax)[1] - 1 + 127, 0) - down, 1)
    scale = np.exp2(byte - 127.0)
    codes = (blocks / scale).astype(np.float32).astype(dtype).astype(np.float64)
    return np.moveaxis((codes * scale).reshape(v.shape), -1, axis)


WIDE = False


def mx_kscale(k):
    if not WIDE:
        return np.ones(k)
    levels = np.array([10, -10, 5, -5, 0])
    if k % 512:
        return np.exp2(np.random.permutation(np.resize(levels, k // 32))).repeat(32)
    a = np.empty((k // 512, 16))
    for p in range(k // 512):
        a[p, :8] = np.random.permutation(np.resize(levels, 8))
        for g in range(8):
            far = levels[np.abs(levels - a[p, g]) >= 10]
            a[p, g + 8] = far[np.random.randint(len(far))]
    return np.exp2(a.ravel()).repeat(32)


def f64(x):
    return np.asarray(x).astype(np.float64)


def striped(idx):
    return np.tile(idx.reshape(-1, 16).T, (8, 1)).astype(np.uint16)


def unstriped(offs):
    return offs[:16].T.reshape(-1).astype(np.int64)


E2M1 = np.array([0.0, 0.5, 1.0, 1.5, 2.0, 3.0, 4.0, 6.0, -0.0, -0.5, -1.0, -1.5, -2.0, -3.0, -4.0, -6.0])


def pack_weight(w, fmt):
    k, n = w.shape
    w = f64(np.asarray(w, np.float32).astype(ml_dtypes.bfloat16)).reshape(k // 32, 32, n)
    amax = np.abs(w).max(1)
    if fmt == "e4m3":
        byte = np.frexp(amax)[1] - 1 + 127 - 7
    else:
        mant, ex = np.frexp(amax / 6.0)
        byte = np.where(mant > 0.5, ex, ex - 1) + 127
    byte = np.clip(np.where(amax > 0, byte, 1), 1, 254)
    scaled = (w * np.exp2(127.0 - byte)[:, None, :]).reshape(k, n).astype(np.float32)
    by_word = np.ascontiguousarray(scaled.reshape(k // 512, 128, 4, n).transpose(0, 1, 3, 2))
    if fmt == "e4m3":
        words = by_word.astype(ml_dtypes.float8_e4m3fn).view(np.uint8)
    else:
        c = by_word.astype(ml_dtypes.float4_e2m1fn).view(np.uint8) & 0xF
        words = (c[..., 0::2] | (c[..., 1::2] << 4)).reshape(k // 512, 128, 2 * n)
    return np.ascontiguousarray(words), np.ascontiguousarray(byte.astype(np.uint8).reshape(k // 512, 16, n))


def unpack_weight(words, scales, fmt):
    g, _, n = scales.shape
    words = np.ascontiguousarray(words).reshape(g, 128, n, -1)
    if fmt == "e4m3":
        vals = words.view(ml_dtypes.float8_e4m3fn).astype(np.float64)
    else:
        nib = np.empty((g, 128, n, 4), np.uint8)
        nib[..., 0::2] = words & 0xF
        nib[..., 1::2] = words >> 4
        vals = E2M1[nib]
    vals = vals * np.repeat(np.exp2(scales.astype(np.float64) - 127.0), 8, axis=1)[..., None]
    return vals.transpose(0, 1, 3, 2).reshape(g * 512, n)


def gelu(v):
    return 0.5 * v * (1.0 + np.tanh(np.sqrt(2.0 / np.pi) * (v + 0.044715 * v**3)))


def bf(x):
    return np.asarray(x, np.float32).astype(ml_dtypes.bfloat16)


def planes(Y):
    n, m = Y.shape
    b = f64(bf(Y)).reshape(n // 32, 32, m)
    amax = np.abs(b).max(1)
    byte = np.clip(np.where(amax > 0, np.frexp(amax)[1] - 1 + 127 - 7, 1), 1, 254)
    codes = (b * np.exp2(127.0 - byte)[:, None, :]).reshape(n, m).astype(np.float32).astype(ml_dtypes.float8_e4m3fn).view(np.uint8)
    words = codes.reshape(n // 512, 128, 4, m).transpose(0, 1, 3, 2)
    return np.ascontiguousarray(words), np.ascontiguousarray(byte.astype(np.uint8).reshape(n // 512, 16, m))


K, H, M, N, T, T3, S = 512, 1024, 512, 512, 2048, 4096, 1024

def setup_inputs():
    n = np.random.standard_normal
    s = mx_kscale(K)[:, None]
    u = mx_kscale(H)[:, None]
    w = mx_kscale(M)[:, None]
    size = np.exp(0.8 * n((1, N)))
    d = {}
    d["tab_words"], d["tab_scales"] = pack_weight(n((K, T)) * s, "e4m3")
    d["tab2_words"], d["tab2_scales"] = pack_weight(n((K, T)) * s, "e4m3")
    d["tab3_words"], d["tab3_scales"] = pack_weight(n((K, T3)) * s, "e2m1")
    d["offs"] = striped(np.random.permutation(T)[:S])
    d["offs2"] = striped(np.random.permutation(T)[:S])
    d["offs3"] = striped(np.random.permutation(T3)[:S])
    d["w1_words"], d["w1_scales"] = pack_weight(n((K, H)) / np.sqrt(K) / s, "e2m1")
    d["w2"] = (1.5 * n((H, M)) / np.sqrt(H) / u).astype(np.float32)
    d["w3"] = (n((K, M)) / np.sqrt(K) / s).astype(np.float32)
    d["w4"] = (1.2 * n((M, N)) / np.sqrt(M) / w * size).astype(np.float32)
    d["w5_words"], d["w5_scales"] = pack_weight(n((K, N)) / np.sqrt(K) / s * size, "e4m3")
    d["g1"] = (np.exp(0.3 * n(H)) * u[:, 0]).astype(np.float32)
    d["b"] = (0.5 * n(M)).astype(np.float32)
    d["g2"] = (np.exp(0.3 * n(M)) * w[:, 0]).astype(np.float32)
    return d

def reference(tab_words, tab_scales, tab2_words, tab2_scales, tab3_words, tab3_scales,
              offs, offs2, offs3, w1_words, w1_scales, w2, w3, w4, w5_words, w5_scales, g1, b, g2):
    v = unpack_weight(tab_words, tab_scales, "e4m3")[:, unstriped(offs)]
    v2 = unpack_weight(tab2_words, tab2_scales, "e4m3")[:, unstriped(offs2)]
    v3 = unpack_weight(tab3_words, tab3_scales, "e2m1")[:, unstriped(offs3)]
    h = f64(g1)[:, None] * np.tanh(unpack_weight(w1_words, w1_scales, "e2m1").T @ v)
    x = (mxq(f64(w2), 0, "e4m3").T @ mxq(h, 0, "e4m3") + mxq(f64(w3), 0, "e4m3").T @ v2) + f64(b)[:, None]
    f = f64(g2)[:, None] * (x / (1.0 + np.exp(-x)))
    y = (mxq(f64(w4), 0, "e4m3").T @ mxq(f, 0, "e4m3")
              + unpack_weight(w5_words, w5_scales, "e4m3").T @ v3)
    words, scales = planes(y)
    return y, words, scales

@@ -1,0 +1,280 @@
+from contextlib import ExitStack
+
+import concourse.mybir as mybir
+
+K, H, M, N, T, T3, S = 512, 1024, 512, 512, 2048, 4096, 1024
+FLOPS = 2 * S * (K * H + H * M + K * M + M * N + K * N)
+
+F32 = mybir.dt.float32
+BF16 = mybir.dt.bfloat16
+I32 = mybir.dt.int32
+U32 = mybir.dt.uint32
+U16 = mybir.dt.uint16
+U8 = mybir.dt.uint8
+E4M3 = mybir.dt.float8_e4m3fn_x4
+E2M1 = mybir.dt.float4_e2m1fn_x4
+ACT = mybir.ActivationFunctionType
+MULT = mybir.AluOpType.mult
+
+P = 128
+PACK = 4
+PASS = P * PACK
+CHUNK = 256
+HALF = 128
+LIST_ROWS = 16
+
+
+def tile_list_ski_push_features_kernel(
+    tc, tab_words, tab_scales, tab2_words, tab2_scales, tab3_words, tab3_scales,
+    offs, offs2, offs3, w1_words, w1_scales, w2, w3, w4, w5_words, w5_scales, g1, b, g2,
+    out_0, out_1, out_2,
+):
+    nc = tc.nc
+    with ExitStack() as ctx:
+        keep = ctx.enter_context(tc.tile_pool(name="keep", bufs=1))
+        ring = ctx.enter_context(tc.tile_pool(name="ring", bufs=2))
+        psum = ctx.enter_context(tc.psum_pool(name="psum", bufs=1))
+
+        def held(name, shape, dtype):
+            return keep.tile(shape, dtype, name=name, align_bytes=64)
+
+        def load_list(name, src):
+            tile = keep.tile([P, S // LIST_ROWS], U16, name=name)
+            nc.sync.dma_start(tile[:], src)
+            return tile
+
+        def load_bytes(name, src, width, dtype, queue):
+            tile = held(name, [P, width], dtype)
+            queue.dma_start(out=tile[:].bitcast(I32), in_=src.bitcast(I32))
+            return tile
+
+        def zeroed_plane(name, width, engine):
+            tile = held(name, [P, width], U8)
+            engine.memset(tile[:].bitcast(I32), 0)
+            return tile
+
+        def load_plane(tile, scales, queues):
+            for q in range(4):
+                queues[q].dma_start(
+                    out=tile[32 * q : 32 * q + 4, :].bitcast(I32),
+                    in_=scales[0, 4 * q : 4 * q + 4, :].bitcast(I32),
+                )
+
+        def gather(name, tag, window, offsets, first, count, dtype):
+            tile = keep.tile([P, count], dtype, name=name, tag=tag, align_bytes=64)
+            cols = slice(first // LIST_ROWS, (first + count) // LIST_ROWS)
+            nc.vector.tensor_copy(tile[:], window[:].indirect(offsets[:, cols]))
+            return tile
+
+        def load_weight(name, rows):
+            raw = held(name, [P, PACK, PASS], F32)
+            nc.sync.dma_start(out=raw[:], in_=rows.rearrange("(p j) c -> p j c", j=PACK))
+            return raw
+
+        def round_weight(name, raw):
+            grouped = held(name, [P, PASS * PACK], BF16)
+            nc.scalar.copy(
+                out=grouped[:].rearrange("p (t m j) -> p m j t", t=PACK, j=PACK),
+                in_=raw[:].rearrange("p j (m t) -> p m j t", t=PACK),
+            )
+            return grouped
+
+        def quantize(name, grouped, width):
+            codes = held(name + "_codes", [P, width], U32)
+            plane = held(name + "_plane", [P, width], U8)
+            nc.vector.quantize_mx(out=codes[:].bitcast(E4M3), scales=plane[:], in_=grouped)
+            return codes, plane
+
+        w1_plane_raw = zeroed_plane("w1_plane_raw", H, nc.vector)
+        tab_plane = zeroed_plane("tab_plane", T, nc.vector)
+        w5_plane_raw = zeroed_plane("w5_plane_raw", N, nc.vector)
+        tab2_plane = zeroed_plane("tab2_plane", T, nc.vector)
+        tab3_plane = zeroed_plane("tab3_plane", T3, nc.vector)
+
+        gain1 = held("gain1", [P, H // PASS, PACK], F32)
+        nc.scalar.dma_start(out=gain1[:], in_=g1.rearrange("(a p t) -> p a t", p=P, t=PACK))
+        list1 = load_list("list1", offs)
+        bias = held("bias", [P, PACK], F32)
+        nc.scalar.dma_start(out=bias[:], in_=b.rearrange("(p t) -> p t", t=PACK))
+        w1_raw = load_bytes("w1_raw", w1_words[0], H, U16, nc.sync)
+        gain2 = held("gain2", [P, PACK], F32)
+        nc.scalar.dma_start(out=gain2[:], in_=g2.rearrange("(p t) -> p t", t=PACK))
+        list2 = load_list("list2", offs2)
+        list3 = load_list("list3", offs3)
+        tab = load_bytes("tab", tab_words[0].rearrange("p t i -> p (t i)"), T, U32, nc.scalar)
+        load_plane(tab_plane, tab_scales, [nc.sync] * 4)
+        load_plane(w1_plane_raw, w1_scales, [nc.gpsimd, nc.gpsimd, nc.sync, nc.sync])
+        w2_raw = [load_weight("w2_raw%d" % a, w2[a * PASS : (a + 1) * PASS, :]) for a in range(H // PASS)]
+        load_plane(tab2_plane, tab2_scales, [nc.sync] * 4)
+        tab2 = load_bytes("tab2", tab2_words[0].rearrange("p t i -> p (t i)"), T, U32, nc.sync)
+        w3_raw = load_weight("w3_raw", w3)
+        w4_raw = load_weight("w4_raw", w4)
+        load_plane(w5_plane_raw, w5_scales, [nc.sync] * 4)
+        w5_raw = load_bytes("w5_raw", w5_words[0].rearrange("p c i -> p (c i)"), N, U32, nc.sync)
+        load_plane(tab3_plane, tab3_scales, [nc.sync] * 4)
+        tab3 = load_bytes("tab3", tab3_words[0], T3, U16, nc.sync)
+
+        warm = held("warm", [P, 8], F32)
+        nc.vector.memset(warm[:, 0:1], 0.0)
+        nc.scalar.activation(out=warm[:, 4:5], in_=warm[:, 0:1], func=ACT.Silu)
+
+        def deal(name, raw, width, dtype):
+            dealt = held(name, [P, width], dtype)
+            nc.vector.tensor_copy(
+                out=dealt[:].rearrange("p (a t m) -> p a t m", t=PACK, m=P),
+                in_=raw.rearrange("p (a m t) -> p a t m", t=PACK, m=P),
+            )
+            return dealt
+
+        w1_codes = deal("w1_codes", w1_raw[:], H, U16)
+        w1_plane = deal("w1_plane", w1_plane_raw[:], H, U8)
+
+        def stage1(c):
+            v_codes = gather("v_codes%d" % c, "v_codes%d" % c, tab, list1, c * CHUNK, CHUNK, U32)
+            v_plane = gather("v_plane%d" % c, "v_plane%d" % c, tab_plane, list1, c * CHUNK, CHUNK, U8)
+            tanh = held("tanh%d" % c, [P, H // PASS, CHUNK, PACK], F32)
+            for u in range(CHUNK // HALF):
+                cols = slice(u * HALF, (u + 1) * HALF)
+                for a in range(H // PASS):
+                    bank = psum.tile([P, PACK, HALF], F32, name="first", tag="first", bufs=4)
+                    for t in range(PACK):
+                        wc = slice(a * PASS + t * P, a * PASS + (t + 1) * P)
+                        nc.tensor.matmul_mx(
+                            out=bank[:, t, :],
+                            lhsT=w1_codes[:, wc].bitcast(E2M1), lhsT_scale=w1_plane[:, wc],
+                            rhs=v_codes[:, cols].bitcast(E4M3), rhs_scale=v_plane[:, cols],
+                            start=True, stop=True,
+                        )
+                    nc.scalar.activation(
+                        out=tanh[:, a, cols, :], in_=bank[:].rearrange("p t n -> p n t"), func=ACT.Tanh,
+                    )
+            return tanh
+
+        def make_h(c, tanh):
+            h = ring.tile([P, H // PASS, CHUNK, PACK], BF16, name="h", align_bytes=64)
+            nc.vector.tensor_tensor(
+                out=h[:], in0=tanh[:],
+                in1=gain1[:].unsqueeze(2).to_broadcast([P, H // PASS, CHUNK, PACK]), op=MULT,
+            )
+            return h
+
+        def stage2(c, h_q, v2_q, w2_q, w3_q):
+            silu = held("silu%d" % c, [P, PACK, CHUNK], F32)
+            for pair in range(2):
+                bank = psum.tile([P, 2, CHUNK], F32, name="second", tag="second", bufs=2)
+                for e in range(2):
+                    t = 2 * pair + e
+                    wc = slice(t * P, (t + 1) * P)
+                    passes = [(w3_q, v2_q[0][:], v2_q[1][:])]
+                    for a in range(H // PASS):
+                        hc = slice(a * CHUNK, (a + 1) * CHUNK)
+                        passes.append((w2_q[a], h_q[0][:, hc], h_q[1][:, hc]))
+                    for i, (w_q, codes, plane) in enumerate(passes):
+                        nc.tensor.matmul_mx(
+                            out=bank[:, e, :],
+                            lhsT=w_q[0][:, wc].bitcast(E4M3), lhsT_scale=w_q[1][:, wc],
+                            rhs=codes.bitcast(E4M3), rhs_scale=plane,
+                            start=(i == 0), stop=(i == len(passes) - 1),
+                        )
+                for e in range(2):
+                    t = 2 * pair + e
+                    nc.scalar.activation(
+                        out=silu[:, t, :], in_=bank[:, e, :], func=ACT.Silu, bias=bias[:, t : t + 1],
+                    )
+            return silu
+
+        def make_f(c, silu):
+            f = ring.tile([P, CHUNK * PACK], BF16, name="f", align_bytes=64)
+            nc.vector.tensor_tensor(
+                out=f[:].rearrange("p (c i t) -> p c t i", i=2, t=PACK),
+                in0=silu[:].rearrange("p t (c i) -> p c t i", i=2),
+                in1=gain2[:].unsqueeze(1).unsqueeze(3).to_broadcast([P, CHUNK // 2, PACK, 2]), op=MULT,
+            )
+            return f
+
+        y_plane = held("y_plane", [P, S], U8)
+
+        def stage3(c, f_q, v3_q, w4_q, w5_q):
+            y = ring.tile([P, PACK, CHUNK], F32, name="y", align_bytes=64)
+            y_round = ring.tile([P, CHUNK, PACK], BF16, name="y_round", align_bytes=64)
+            for u in range(CHUNK // HALF):
+                cols = slice(u * HALF, (u + 1) * HALF)
+                first = (c * CHUNK + u * HALF) % PASS
+                v3_cols = slice(first, first + HALF)
+                bank = psum.tile([P, PACK, HALF], F32, name="third", tag="third", bufs=2)
+                for t in range(PACK):
+                    wc = slice(t * P, (t + 1) * P)
+                    nc.tensor.matmul_mx(
+                        out=bank[:, t, :],
+                        lhsT=w5_q[0][:, wc].bitcast(E4M3), lhsT_scale=w5_q[1][:, wc],
+                        rhs=v3_q[0][:, v3_cols].bitcast(E2M1), rhs_scale=v3_q[1][:, v3_cols],
+                        start=True, stop=False,
+                    )
+                    nc.tensor.matmul_mx(
+                        out=bank[:, t, :],
+                        lhsT=w4_q[0][:, wc].bitcast(E4M3), lhsT_scale=w4_q[1][:, wc],
+                        rhs=f_q[0][:, cols].bitcast(E4M3), rhs_scale=f_q[1][:, cols],
+                        start=False, stop=True,
+                    )
+                nc.scalar.copy(out=y_round[:, cols, :], in_=bank[:].rearrange("p t n -> p n t"))
+                nc.scalar.copy(out=y[:, :, cols], in_=bank[:])
+            all_cols = slice(c * CHUNK, (c + 1) * CHUNK)
+            y_codes = held("y_codes%d" % c, [P, CHUNK], U32)
+            nc.vector.quantize_mx(
+                out=y_codes[:].bitcast(E4M3), scales=y_plane[:, all_cols],
+                in_=y_round[:].rearrange("p n t -> p (n t)"),
+            )
+            nc.sync.dma_start(out=out_0.rearrange("(p t) n -> p t n", t=PACK)[:, :, all_cols], in_=y[:])
+            nc.sync.dma_start(
+                out=out_1[0].rearrange("p m t -> p (m t)").bitcast(I32)[:, all_cols], in_=y_codes[:].bitcast(I32),
+            )
+
+        def h_quant(c, tanh):
+            h = make_h(c, tanh)
+            return quantize("h%d" % c, h[:].rearrange("p a n t -> p (a n t)"), 2 * CHUNK)
+
+        def gather2(c):
+            return (gather("v2_codes%d" % c, "late_codes%d" % c, tab2, list2, c * CHUNK, CHUNK, U32),
+                    gather("v2_plane%d" % c, "late_plane%d" % c, tab2_plane, list2, c * CHUNK, CHUNK, U8))
+
+        def gather3(c):
+            return (gather("v3_codes%d" % c, "late_codes%d" % c, tab3, list3, c * CHUNK, PASS, U16),
+                    gather("v3_plane%d" % c, "late_plane%d" % c, tab3_plane, list3, c * CHUNK, PASS, U8))
+
+        def f_quant(c, silu):
+            return quantize("f%d" % c, make_f(c, silu)[:], CHUNK)
+
+        tanh = [stage1(0), stage1(1)]
+        w2_round = [round_weight("w2_round%d" % a, w2_raw[a]) for a in range(H // PASS)]
+        w3_round = round_weight("w3_round", w3_raw)
+        tanh.append(stage1(2))
+        h_q = [h_quant(0, tanh[0]), h_quant(1, tanh[1])]
+        v2_q = [gather2(0), gather2(1)]
+        w2_q = [quantize("w2_%d" % a, w2_round[a][:], PASS) for a in range(H // PASS)]
+        w3_q = quantize("w3", w3_round[:], PASS)
+        silu0 = stage2(0, h_q[0], v2_q[0], w2_q, w3_q)
+        v2_q.extend([gather2(2), gather2(3)])
+        w4_round = round_weight("w4_round", w4_raw)
+        tanh.append(stage1(3))
+        silu1 = stage2(1, h_q[1], v2_q[1], w2_q, w3_q)
+        h_q.append(h_quant(2, tanh[2]))
+        f0 = f_quant(0, silu0)
+        w4_q = quantize("w4", w4_round[:], PASS)
+        w5_q = (deal("w5_codes", w5_raw[:].bitcast(I32), N, I32), deal("w5_plane", w5_plane_raw[:], N, U8))
+        v3_low = gather3(0)
+        stage3(0, f0, v3_low, w4_q, w5_q)
+        silu2 = stage2(2, h_q[2], v2_q[2], w2_q, w3_q)
+        h_q.append(h_quant(3, tanh[3]))
+        f1 = f_quant(1, silu1)
+        stage3(1, f1, v3_low, w4_q, w5_q)
+        silu3 = stage2(3, h_q[3], v2_q[3], w2_q, w3_q)
+        v3_high = gather3(2)
+        stage3(2, f_quant(2, silu2), v3_high, w4_q, w5_q)
+        stage3(3, f_quant(3, silu3), v3_high, w4_q, w5_q)
+
+        for q in range(4):
+            queue = nc.sync if q % 2 == 0 else nc.scalar
+            queue.dma_start(
+                out=out_2[0, 4 * q : 4 * q + 4, :].bitcast(I32),
+                in_=y_plane[32 * q : 32 * q + 4, :].bitcast(I32),
+            )

@@ -32,24 +32,26 @@ def tile_list_ski_push_features_kernel(
     nc = tc.nc
     with ExitStack() as ctx:
         keep = ctx.enter_context(tc.tile_pool(name="keep", bufs=1))
-        ring = ctx.enter_context(tc.tile_pool(name="ring", bufs=2))
+        reuse = ctx.enter_context(tc.tile_pool(name="reuse", bufs=1))
         psum = ctx.enter_context(tc.psum_pool(name="psum", bufs=1))
 
-        def held(name, shape, dtype):
-            return keep.tile(shape, dtype, name=name, align_bytes=64)
+        def held(name, shape, dtype, place=None):
+            if isinstance(place, int):
+                return reuse.tile(shape, dtype, name=name, align_bytes=64, offset=place)
+            return keep.tile(shape, dtype, name=name, tag=place or name, align_bytes=64)
 
         def load_list(name, src):
             tile = keep.tile([P, S // LIST_ROWS], U16, name=name)
             nc.sync.dma_start(tile[:], src)
             return tile
 
-        def load_bytes(name, src, width, dtype, queue):
-            tile = held(name, [P, width], dtype)
-            queue.dma_start(out=tile[:].bitcast(I32), in_=src.bitcast(I32))
+        def load_bytes(name, tag, src, width, dtype):
+            tile = keep.tile([P, width], dtype, name=name, tag=tag, align_bytes=64)
+            nc.sync.dma_start(out=tile[:].bitcast(I32), in_=src.bitcast(I32))
             return tile
 
-        def zeroed_plane(name, width, engine):
-            tile = held(name, [P, width], U8)
+        def zeroed_plane(name, tag, width, engine):
+            tile = keep.tile([P, width], U8, name=name, tag=tag, align_bytes=64)
             engine.memset(tile[:].bitcast(I32), 0)
             return tile
 
@@ -61,18 +63,18 @@ def tile_list_ski_push_features_kernel(
                 )
 
         def gather(name, tag, window, offsets, first, count, dtype):
-            tile = keep.tile([P, count], dtype, name=name, tag=tag, align_bytes=64)
+            tile = held(name, [P, count], dtype, tag)
             cols = slice(first // LIST_ROWS, (first + count) // LIST_ROWS)
             nc.vector.tensor_copy(tile[:], window[:].indirect(offsets[:, cols]))
             return tile
 
-        def load_weight(name, rows):
-            raw = held(name, [P, PACK, PASS], F32)
+        def load_weight(name, tag, rows):
+            raw = keep.tile([P, PACK, PASS], F32, name=name, tag=tag, align_bytes=64)
             nc.sync.dma_start(out=raw[:], in_=rows.rearrange("(p j) c -> p j c", j=PACK))
             return raw
 
-        def round_weight(name, raw):
-            grouped = held(name, [P, PASS * PACK], BF16)
+        def round_weight(name, raw, place=None):
+            grouped = held(name, [P, PASS * PACK], BF16, place)
             nc.scalar.copy(
                 out=grouped[:].rearrange("p (t m j) -> p m j t", t=PACK, j=PACK),
                 in_=raw[:].rearrange("p j (m t) -> p m j t", t=PACK),
@@ -85,58 +87,47 @@ def tile_list_ski_push_features_kernel(
             nc.vector.quantize_mx(out=codes[:].bitcast(E4M3), scales=plane[:], in_=grouped)
             return codes, plane
 
-        w1_plane_raw = zeroed_plane("w1_plane_raw", H, nc.vector)
-        tab_plane = zeroed_plane("tab_plane", T, nc.vector)
-        w5_plane_raw = zeroed_plane("w5_plane_raw", N, nc.vector)
-        tab2_plane = zeroed_plane("tab2_plane", T, nc.vector)
-        tab3_plane = zeroed_plane("tab3_plane", T3, nc.vector)
+        w1_plane_raw = zeroed_plane("w1_plane_raw", "slot1", H, nc.vector)
+        tab_plane = zeroed_plane("tab_plane", "tab_plane", T, nc.vector)
+        tab2_plane = zeroed_plane("tab2_plane", "tab2_plane", T, nc.vector)
 
-        gain1 = held("gain1", [P, H // PASS, PACK], F32)
-        nc.scalar.dma_start(out=gain1[:], in_=g1.rearrange("(a p t) -> p a t", p=P, t=PACK))
         list1 = load_list("list1", offs)
-        bias = held("bias", [P, PACK], F32)
-        nc.scalar.dma_start(out=bias[:], in_=b.rearrange("(p t) -> p t", t=PACK))
-        w1_raw = load_bytes("w1_raw", w1_words[0], H, U16, nc.sync)
-        gain2 = held("gain2", [P, PACK], F32)
-        nc.scalar.dma_start(out=gain2[:], in_=g2.rearrange("(p t) -> p t", t=PACK))
+        w1_raw = load_bytes("w1_raw", "slot0", w1_words[0], H, U16)
         list2 = load_list("list2", offs2)
         list3 = load_list("list3", offs3)
-        tab = load_bytes("tab", tab_words[0].rearrange("p t i -> p (t i)"), T, U32, nc.scalar)
-        load_plane(tab_plane, tab_scales, [nc.sync] * 4)
-        load_plane(w1_plane_raw, w1_scales, [nc.gpsimd, nc.gpsimd, nc.sync, nc.sync])
-        w2_raw = [load_weight("w2_raw%d" % a, w2[a * PASS : (a + 1) * PASS, :]) for a in range(H // PASS)]
-        load_plane(tab2_plane, tab2_scales, [nc.sync] * 4)
-        tab2 = load_bytes("tab2", tab2_words[0].rearrange("p t i -> p (t i)"), T, U32, nc.sync)
-        w3_raw = load_weight("w3_raw", w3)
-        w4_raw = load_weight("w4_raw", w4)
-        load_plane(w5_plane_raw, w5_scales, [nc.sync] * 4)
-        w5_raw = load_bytes("w5_raw", w5_words[0].rearrange("p c i -> p (c i)"), N, U32, nc.sync)
-        load_plane(tab3_plane, tab3_scales, [nc.sync] * 4)
-        tab3 = load_bytes("tab3", tab3_words[0], T3, U16, nc.sync)
+        tab = load_bytes("tab", "tab", tab_words[0].rearrange("p t i -> p (t i)"), T, U32)
+        load_plane(w1_plane_raw, w1_scales, [nc.gpsimd, nc.scalar, nc.scalar, nc.scalar])
+        load_plane(tab_plane, tab_scales, [nc.scalar] * 4)
 
-        warm = held("warm", [P, 8], F32)
-        nc.vector.memset(warm[:, 0:1], 0.0)
-        nc.scalar.activation(out=warm[:, 4:5], in_=warm[:, 0:1], func=ACT.Silu)
+        warm_in = keep.tile([P, 1], F32, name="warm_in", tag="small0", align_bytes=64)
+        warm_out = keep.tile([P, 1], F32, name="warm_out", tag="small1", align_bytes=64)
+        nc.vector.memset(warm_in[:], 0.0)
+        nc.scalar.activation(out=warm_out[:], in_=warm_in[:], func=ACT.Silu)
+        vectors = keep.tile([P, 3, 16], F32, name="vectors", tag="small0", align_bytes=64)
+        gain1 = vectors[:, 0, 0:8].rearrange("p (a t) -> p a t", t=PACK)
+        bias = vectors[:, 1, 0:PACK]
+        gain2 = vectors[:, 2, 0:PACK]
+        nc.sync.dma_start(out=gain1, in_=g1.rearrange("(a p t) -> p a t", p=P, t=PACK))
+        nc.sync.dma_start(out=bias, in_=b.rearrange("(p t) -> p t", t=PACK))
+        nc.sync.dma_start(out=gain2, in_=g2.rearrange("(p t) -> p t", t=PACK))
 
-        def deal(name, raw, width, dtype):
-            dealt = held(name, [P, width], dtype)
+        def deal(name, tag, raw, width, dtype):
+            dealt = keep.tile([P, width], dtype, name=name, tag=tag, align_bytes=64)
             nc.vector.tensor_copy(
-                out=dealt[:].rearrange("p (a t m) -> p a t m", t=PACK, m=P),
-                in_=raw.rearrange("p (a m t) -> p a t m", t=PACK, m=P),
+                out=dealt[:].rearrange("p (a t m) -> p a m t", t=PACK, m=P),
+                in_=raw.rearrange("p (a m t) -> p a m t", t=PACK, m=P),
             )
             return dealt
 
-        w1_codes = deal("w1_codes", w1_raw[:], H, U16)
-        w1_plane = deal("w1_plane", w1_plane_raw[:], H, U8)
+        w1_codes = deal("w1_codes", "w1_codes", w1_raw[:], H, U16)
+        w1_plane = deal("w1_plane", "w1_plane", w1_plane_raw[:], H, U8)
 
-        def stage1(c):
-            v_codes = gather("v_codes%d" % c, "v_codes%d" % c, tab, list1, c * CHUNK, CHUNK, U32)
-            v_plane = gather("v_plane%d" % c, "v_plane%d" % c, tab_plane, list1, c * CHUNK, CHUNK, U8)
-            tanh = held("tanh%d" % c, [P, H // PASS, CHUNK, PACK], F32)
+        def stage1(c, v_codes, v_plane, place=None):
+            tanh = held("tanh%d" % c, [P, H // PASS, CHUNK, PACK], F32, place)
             for u in range(CHUNK // HALF):
                 cols = slice(u * HALF, (u + 1) * HALF)
                 for a in range(H // PASS):
-                    bank = psum.tile([P, PACK, HALF], F32, name="first", tag="first", bufs=4)
+                    bank = psum.tile([P, PACK, HALF], F32, name="first", tag="first", bufs=5)
                     for t in range(PACK):
                         wc = slice(a * PASS + t * P, a * PASS + (t + 1) * P)
                         nc.tensor.matmul_mx(
@@ -150,22 +141,29 @@ def tile_list_ski_push_features_kernel(
                     )
             return tanh
 
-        def make_h(c, tanh):
-            h = ring.tile([P, H // PASS, CHUNK, PACK], BF16, name="h", align_bytes=64)
-            nc.vector.tensor_tensor(
-                out=h[:], in0=tanh[:],
-                in1=gain1[:].unsqueeze(2).to_broadcast([P, H // PASS, CHUNK, PACK]), op=MULT,
-            )
+        def make_h(c, place, tanh, on_gpsimd):
+            h = held("h%d" % c, [P, H // PASS, CHUNK, PACK], BF16, place)
+            if on_gpsimd:
+                for a in range(H // PASS):
+                    nc.gpsimd.tensor_tensor(
+                        out=h[:, a, :, :], in0=tanh[:, a, :, :],
+                        in1=gain1[:, a, :].unsqueeze(1).to_broadcast([P, CHUNK, PACK]), op=MULT,
+                    )
+            else:
+                nc.vector.tensor_tensor(
+                    out=h[:], in0=tanh[:],
+                    in1=gain1.unsqueeze(2).to_broadcast([P, H // PASS, CHUNK, PACK]), op=MULT,
+                )
             return h
 
         def stage2(c, h_q, v2_q, w2_q, w3_q):
             silu = held("silu%d" % c, [P, PACK, CHUNK], F32)
             for pair in range(2):
-                bank = psum.tile([P, 2, CHUNK], F32, name="second", tag="second", bufs=2)
+                bank = psum.tile([P, 2, CHUNK], F32, name="second", tag="second", bufs=3)
                 for e in range(2):
                     t = 2 * pair + e
                     wc = slice(t * P, (t + 1) * P)
-                    passes = [(w3_q, v2_q[0][:], v2_q[1][:])]
+                    passes = [(w3_q, v2_q[0], v2_q[1])]
                     for a in range(H // PASS):
                         hc = slice(a * CHUNK, (a + 1) * CHUNK)
                         passes.append((w2_q[a], h_q[0][:, hc], h_q[1][:, hc]))
@@ -184,40 +182,41 @@ def tile_list_ski_push_features_kernel(
             return silu
 
         def make_f(c, silu):
-            f = ring.tile([P, CHUNK * PACK], BF16, name="f", align_bytes=64)
+            f = held("f%d" % c, [P, CHUNK * PACK], BF16)
             nc.vector.tensor_tensor(
                 out=f[:].rearrange("p (c i t) -> p c t i", i=2, t=PACK),
                 in0=silu[:].rearrange("p t (c i) -> p c t i", i=2),
-                in1=gain2[:].unsqueeze(1).unsqueeze(3).to_broadcast([P, CHUNK // 2, PACK, 2]), op=MULT,
+                in1=gain2.unsqueeze(1).unsqueeze(3).to_broadcast([P, CHUNK // 2, PACK, 2]), op=MULT,
             )
             return f
 
         y_plane = held("y_plane", [P, S], U8)
 
-        def stage3(c, f_q, v3_q, w4_q, w5_q):
-            y = ring.tile([P, PACK, CHUNK], F32, name="y", align_bytes=64)
-            y_round = ring.tile([P, CHUNK, PACK], BF16, name="y_round", align_bytes=64)
+        def stage3(c, f_q, v3_q, w4_q, w5_q, shared):
+            y = held("y%d" % c, [P, PACK, CHUNK], F32)
+            y_round = held("y_round%d" % c, [P, CHUNK, PACK], BF16)
             for u in range(CHUNK // HALF):
                 cols = slice(u * HALF, (u + 1) * HALF)
-                first = (c * CHUNK + u * HALF) % PASS
+                first = c * CHUNK + u * HALF
                 v3_cols = slice(first, first + HALF)
-                bank = psum.tile([P, PACK, HALF], F32, name="third", tag="third", bufs=2)
+                bank = psum.tile([P, PACK, HALF], F32, name="third", tag="first", bufs=5)
                 for t in range(PACK):
                     wc = slice(t * P, (t + 1) * P)
                     nc.tensor.matmul_mx(
                         out=bank[:, t, :],
-                        lhsT=w5_q[0][:, wc].bitcast(E4M3), lhsT_scale=w5_q[1][:, wc],
-                        rhs=v3_q[0][:, v3_cols].bitcast(E2M1), rhs_scale=v3_q[1][:, v3_cols],
+                        lhsT=w4_q[0][:, wc].bitcast(E4M3), lhsT_scale=w4_q[1][:, wc],
+                        rhs=f_q[0][:, cols].bitcast(E4M3), rhs_scale=f_q[1][:, cols],
                         start=True, stop=False,
                     )
                     nc.tensor.matmul_mx(
                         out=bank[:, t, :],
-                        lhsT=w4_q[0][:, wc].bitcast(E4M3), lhsT_scale=w4_q[1][:, wc],
-                        rhs=f_q[0][:, cols].bitcast(E4M3), rhs_scale=f_q[1][:, cols],
+                        lhsT=w5_q[0][:, wc].bitcast(E4M3), lhsT_scale=w5_q[1][:, wc],
+                        rhs=v3_q[0][:, v3_cols].bitcast(E2M1), rhs_scale=v3_q[1][:, v3_cols],
                         start=False, stop=True,
                     )
-                nc.scalar.copy(out=y_round[:, cols, :], in_=bank[:].rearrange("p t n -> p n t"))
-                nc.scalar.copy(out=y[:, :, cols], in_=bank[:])
+                copy = nc.vector.tensor_copy if (shared and u == 1) else nc.scalar.copy
+                copy(out=y[:, :, cols], in_=bank[:])
+                copy(out=y_round[:, cols, :], in_=bank[:].rearrange("p t n -> p n t"))
             all_cols = slice(c * CHUNK, (c + 1) * CHUNK)
             y_codes = held("y_codes%d" % c, [P, CHUNK], U32)
             nc.vector.quantize_mx(
@@ -229,48 +228,69 @@ def tile_list_ski_push_features_kernel(
                 out=out_1[0].rearrange("p m t -> p (m t)").bitcast(I32)[:, all_cols], in_=y_codes[:].bitcast(I32),
             )
 
-        def h_quant(c, tanh):
-            h = make_h(c, tanh)
+        def h_quant(c, h):
             return quantize("h%d" % c, h[:].rearrange("p a n t -> p (a n t)"), 2 * CHUNK)
 
-        def gather2(c):
-            return (gather("v2_codes%d" % c, "late_codes%d" % c, tab2, list2, c * CHUNK, CHUNK, U32),
-                    gather("v2_plane%d" % c, "late_plane%d" % c, tab2_plane, list2, c * CHUNK, CHUNK, U8))
+        def gather_pair(name, tags, words, plane, offsets, first, count, dtype):
+            return (gather(name + "_codes", tags[0], words, offsets, first, count, dtype),
+                    gather(name + "_plane", tags[1], plane, offsets, first, count, U8))
 
-        def gather3(c):
-            return (gather("v3_codes%d" % c, "late_codes%d" % c, tab3, list3, c * CHUNK, PASS, U16),
-                    gather("v3_plane%d" % c, "late_plane%d" % c, tab3_plane, list3, c * CHUNK, PASS, U8))
+        def part(pair, i):
+            cols = slice(i * CHUNK, (i + 1) * CHUNK)
+            return pair[0][:, cols], pair[1][:, cols]
 
         def f_quant(c, silu):
             return quantize("f%d" % c, make_f(c, silu)[:], CHUNK)
 
-        tanh = [stage1(0), stage1(1)]
-        w2_round = [round_weight("w2_round%d" % a, w2_raw[a]) for a in range(H // PASS)]
-        w3_round = round_weight("w3_round", w3_raw)
-        tanh.append(stage1(2))
-        h_q = [h_quant(0, tanh[0]), h_quant(1, tanh[1])]
-        v2_q = [gather2(0), gather2(1)]
+        v_0 = gather_pair("v_0", ("v_0_codes", "v_0_plane"), tab, tab_plane, list1, 0, CHUNK, U32)
+        tanh0 = stage1(0, *part(v_0, 0), 0)
+        v_1 = gather_pair("v_1", ("slot1", "v_1_plane"), tab, tab_plane, list1, CHUNK, CHUNK, U32)
+        tanh1 = stage1(1, *part(v_1, 0))
+        v_high = gather_pair("v_high", ("v_0_codes", "v_high_plane"), tab, tab_plane, list1, PASS, PASS, U32)
+
+        w2_raw0 = load_weight("w2_raw0", "slot0", w2[:PASS, :])
+        load_plane(tab2_plane, tab2_scales, [nc.sync] * 4)
+        tab2 = load_bytes("tab2", "small1", tab2_words[0].rearrange("p t i -> p (t i)"), T, U32)
+        w2_raw1 = load_weight("w2_raw1", "v_0_plane", w2[PASS:, :])
+        w3_raw = load_weight("w3_raw", "v_1_plane", w3)
+        tab3 = load_bytes("tab3", "slot1", tab3_words[0], T3, U16)
+        tab3_plane = zeroed_plane("tab3_plane", "tab_plane", T3, nc.gpsimd)
+        w5_plane_raw = zeroed_plane("w5_plane_raw", "tab", N, nc.gpsimd)
+        load_plane(tab3_plane, tab3_scales, [nc.sync] * 4)
+
+        w2_round = [round_weight("w2_round0", w2_raw0), round_weight("w2_round1", w2_raw1)]
+        w4_raw = load_weight("w4_raw", "slot0", w4)
+        load_plane(w5_plane_raw, w5_scales, [nc.sync] * 4)
+        w5_raw = load_bytes("w5_raw", "v_0_plane", w5_words[0].rearrange("p c i -> p (c i)"), N, U32)
+        tanh2 = stage1(2, *part(v_high, 0))
+        w3_round = round_weight("w3_round", w3_raw, 10240)
+        h0_round = make_h(0, None, tanh0, False)
+        h1_round = make_h(1, 5120, tanh1, True)
+        v2 = gather_pair("v2", (0, 4096), tab2, tab2_plane, list2, 0, S, U32)
+        h0 = h_quant(0, h0_round)
+        h1 = h_quant(1, h1_round)
         w2_q = [quantize("w2_%d" % a, w2_round[a][:], PASS) for a in range(H // PASS)]
+        h2 = h_quant(2, make_h(2, None, tanh2, False))
         w3_q = quantize("w3", w3_round[:], PASS)
-        silu0 = stage2(0, h_q[0], v2_q[0], w2_q, w3_q)
-        v2_q.extend([gather2(2), gather2(3)])
+        tanh3 = stage1(3, *part(v_high, 1))
         w4_round = round_weight("w4_round", w4_raw)
-        tanh.append(stage1(3))
-        silu1 = stage2(1, h_q[1], v2_q[1], w2_q, w3_q)
-        h_q.append(h_quant(2, tanh[2]))
-        f0 = f_quant(0, silu0)
+        silu0 = stage2(0, h0, part(v2, 0), w2_q, w3_q)
+        silu1 = stage2(1, h1, part(v2, 1), w2_q, w3_q)
+        silu2 = stage2(2, h2, part(v2, 2), w2_q, w3_q)
+        h3_round = make_h(3, 13312, tanh3, True)
+        v3 = gather_pair("v3", (10240, 12288), tab3, tab3_plane, list3, 0, S, U16)
+        w5_q = (deal("w5_codes", "w5_codes", w5_raw[:].bitcast(I32), N, I32), deal("w5_plane", "w5_plane", w5_plane_raw[:], N, U8))
         w4_q = quantize("w4", w4_round[:], PASS)
-        w5_q = (deal("w5_codes", w5_raw[:].bitcast(I32), N, I32), deal("w5_plane", w5_plane_raw[:], N, U8))
-        v3_low = gather3(0)
-        stage3(0, f0, v3_low, w4_q, w5_q)
-        silu2 = stage2(2, h_q[2], v2_q[2], w2_q, w3_q)
-        h_q.append(h_quant(3, tanh[3]))
+        f0 = f_quant(0, silu0)
+        h3 = h_quant(3, h3_round)
+        stage3(0, f0, v3, w4_q, w5_q, False)
+        silu3 = stage2(3, h3, part(v2, 3), w2_q, w3_q)
         f1 = f_quant(1, silu1)
-        stage3(1, f1, v3_low, w4_q, w5_q)
-        silu3 = stage2(3, h_q[3], v2_q[3], w2_q, w3_q)
-        v3_high = gather3(2)
-        stage3(2, f_quant(2, silu2), v3_high, w4_q, w5_q)
-        stage3(3, f_quant(3, silu3), v3_high, w4_q, w5_q)
+        f2 = f_quant(2, silu2)
+        stage3(1, f1, v3, w4_q, w5_q, False)
+        f3 = f_quant(3, silu3)
+        stage3(2, f2, v3, w4_q, w5_q, True)
+        stage3(3, f3, v3, w4_q, w5_q, True)
 
         for q in range(4):
             queue = nc.sync if q % 2 == 0 else nc.scalar

@@ -15,6 +15,7 @@ E4M3 = mybir.dt.float8_e4m3fn_x4
 E2M1 = mybir.dt.float4_e2m1fn_x4
 ACT = mybir.ActivationFunctionType
 MULT = mybir.AluOpType.mult
+ADD = mybir.AluOpType.add
 
 P = 128
 PACK = 4
@@ -45,13 +46,13 @@ def tile_list_ski_push_features_kernel(
             nc.sync.dma_start(tile[:], src)
             return tile
 
-        def load_bytes(name, tag, src, width, dtype):
-            tile = keep.tile([P, width], dtype, name=name, tag=tag, align_bytes=64)
-            nc.sync.dma_start(out=tile[:].bitcast(I32), in_=src.bitcast(I32))
+        def load_bytes(name, tag, src, width, dtype, queue=nc.sync):
+            tile = held(name, [P, width], dtype, tag)
+            queue.dma_start(out=tile[:].bitcast(I32), in_=src.bitcast(I32))
             return tile
 
         def zeroed_plane(name, tag, width, engine):
-            tile = keep.tile([P, width], U8, name=name, tag=tag, align_bytes=64)
+            tile = held(name, [P, width], U8, tag)
             engine.memset(tile[:].bitcast(I32), 0)
             return tile
 
@@ -68,51 +69,52 @@ def tile_list_ski_push_features_kernel(
             nc.vector.tensor_copy(tile[:], window[:].indirect(offsets[:, cols]))
             return tile
 
-        def load_weight(name, tag, rows):
-            raw = keep.tile([P, PACK, PASS], F32, name=name, tag=tag, align_bytes=64)
-            nc.sync.dma_start(out=raw[:], in_=rows.rearrange("(p j) c -> p j c", j=PACK))
+        def load_weight(name, tag, rows, queue=nc.sync):
+            raw = held(name, [P, PACK, PASS], F32, tag)
+            queue.dma_start(out=raw[:], in_=rows.rearrange("(p j) c -> p j c", j=PACK))
             return raw
 
-        def round_weight(name, raw, place=None):
+        def round_weight(name, raw, place=None, on_gpsimd=False):
             grouped = held(name, [P, PASS * PACK], BF16, place)
-            nc.scalar.copy(
-                out=grouped[:].rearrange("p (t m j) -> p m j t", t=PACK, j=PACK),
-                in_=raw[:].rearrange("p j (m t) -> p m j t", t=PACK),
-            )
+            dst = grouped[:].rearrange("p (t m j) -> p m j t", t=PACK, j=PACK)
+            src = raw[:].rearrange("p j (m t) -> p m j t", t=PACK)
+            if on_gpsimd:
+                nc.gpsimd.tensor_scalar(out=dst, in0=src, scalar1=1.0, scalar2=0.0, op0=MULT, op1=ADD)
+            else:
+                nc.scalar.copy(out=dst, in_=src)
             return grouped
 
-        def quantize(name, grouped, width):
-            codes = held(name + "_codes", [P, width], U32)
-            plane = held(name + "_plane", [P, width], U8)
+        def quantize(name, grouped, width, place=None, plane_place=None):
+            codes = held(name + "_codes", [P, width], U32, place)
+            plane = held(name + "_plane", [P, width], U8, plane_place)
             nc.vector.quantize_mx(out=codes[:].bitcast(E4M3), scales=plane[:], in_=grouped)
             return codes, plane
 
-        w1_plane_raw = zeroed_plane("w1_plane_raw", "slot1", H, nc.vector)
+        w1_plane_raw = zeroed_plane("w1_plane_raw", 33536, H, nc.vector)
         tab_plane = zeroed_plane("tab_plane", "tab_plane", T, nc.vector)
-        tab2_plane = zeroed_plane("tab2_plane", "tab2_plane", T, nc.vector)
 
         list1 = load_list("list1", offs)
-        w1_raw = load_bytes("w1_raw", "slot0", w1_words[0], H, U16)
+        w1_raw = load_bytes("w1_raw", 49664, w1_words[0], H, U16)
         list2 = load_list("list2", offs2)
         list3 = load_list("list3", offs3)
         tab = load_bytes("tab", "tab", tab_words[0].rearrange("p t i -> p (t i)"), T, U32)
         load_plane(w1_plane_raw, w1_scales, [nc.gpsimd, nc.scalar, nc.scalar, nc.scalar])
         load_plane(tab_plane, tab_scales, [nc.scalar] * 4)
 
-        warm_in = keep.tile([P, 1], F32, name="warm_in", tag="small0", align_bytes=64)
-        warm_out = keep.tile([P, 1], F32, name="warm_out", tag="small1", align_bytes=64)
+        warm_in = held("warm_in", [P, 32], F32, 56768)
+        warm_out = held("warm_out", [P, 32], F32, 25472)
         nc.vector.memset(warm_in[:], 0.0)
         nc.scalar.activation(out=warm_out[:], in_=warm_in[:], func=ACT.Silu)
-        vectors = keep.tile([P, 3, 16], F32, name="vectors", tag="small0", align_bytes=64)
+        vectors = held("vectors", [P, 3, 16], F32, 56832)
         gain1 = vectors[:, 0, 0:8].rearrange("p (a t) -> p a t", t=PACK)
         bias = vectors[:, 1, 0:PACK]
         gain2 = vectors[:, 2, 0:PACK]
-        nc.sync.dma_start(out=gain1, in_=g1.rearrange("(a p t) -> p a t", p=P, t=PACK))
-        nc.sync.dma_start(out=bias, in_=b.rearrange("(p t) -> p t", t=PACK))
-        nc.sync.dma_start(out=gain2, in_=g2.rearrange("(p t) -> p t", t=PACK))
+        nc.scalar.dma_start(out=gain1, in_=g1.rearrange("(a p t) -> p a t", p=P, t=PACK))
+        nc.scalar.dma_start(out=bias, in_=b.rearrange("(p t) -> p t", t=PACK))
+        nc.scalar.dma_start(out=gain2, in_=g2.rearrange("(p t) -> p t", t=PACK))
 
         def deal(name, tag, raw, width, dtype):
-            dealt = keep.tile([P, width], dtype, name=name, tag=tag, align_bytes=64)
+            dealt = held(name, [P, width], dtype, tag)
             nc.vector.tensor_copy(
                 out=dealt[:].rearrange("p (a t m) -> p a m t", t=PACK, m=P),
                 in_=raw.rearrange("p (a m t) -> p a m t", t=PACK, m=P),
@@ -127,7 +129,7 @@ def tile_list_ski_push_features_kernel(
             for u in range(CHUNK // HALF):
                 cols = slice(u * HALF, (u + 1) * HALF)
                 for a in range(H // PASS):
-                    bank = psum.tile([P, PACK, HALF], F32, name="first", tag="first", bufs=5)
+                    bank = psum.tile([P, PACK, HALF], F32, name="first", tag="bank", bufs=8)
                     for t in range(PACK):
                         wc = slice(a * PASS + t * P, a * PASS + (t + 1) * P)
                         nc.tensor.matmul_mx(
@@ -159,7 +161,7 @@ def tile_list_ski_push_features_kernel(
         def stage2(c, h_q, v2_q, w2_q, w3_q):
             silu = held("silu%d" % c, [P, PACK, CHUNK], F32)
             for pair in range(2):
-                bank = psum.tile([P, 2, CHUNK], F32, name="second", tag="second", bufs=3)
+                bank = psum.tile([P, 2, CHUNK], F32, name="second", tag="bank", bufs=8)
                 for e in range(2):
                     t = 2 * pair + e
                     wc = slice(t * P, (t + 1) * P)
@@ -181,25 +183,24 @@ def tile_list_ski_push_features_kernel(
                     )
             return silu
 
-        def make_f(c, silu):
-            f = held("f%d" % c, [P, CHUNK * PACK], BF16)
+        def make_f(c, silu, place=None):
+            f = held("f%d" % c, [P, CHUNK * PACK], BF16, place)
             nc.vector.tensor_tensor(
-                out=f[:].rearrange("p (c i t) -> p c t i", i=2, t=PACK),
-                in0=silu[:].rearrange("p t (c i) -> p c t i", i=2),
-                in1=gain2.unsqueeze(1).unsqueeze(3).to_broadcast([P, CHUNK // 2, PACK, 2]), op=MULT,
+                out=f[:].rearrange("p (c i t) -> p c t i", i=PACK, t=PACK),
+                in0=silu[:].rearrange("p t (c i) -> p c t i", i=PACK),
+                in1=gain2.unsqueeze(1).unsqueeze(3).to_broadcast([P, CHUNK // PACK, PACK, PACK]), op=MULT,
             )
             return f
 
         y_plane = held("y_plane", [P, S], U8)
 
-        def stage3(c, f_q, v3_q, w4_q, w5_q, shared):
+        def stage3(c, f_q, v3_q, w4_q, w5_q):
             y = held("y%d" % c, [P, PACK, CHUNK], F32)
-            y_round = held("y_round%d" % c, [P, CHUNK, PACK], BF16)
             for u in range(CHUNK // HALF):
                 cols = slice(u * HALF, (u + 1) * HALF)
                 first = c * CHUNK + u * HALF
                 v3_cols = slice(first, first + HALF)
-                bank = psum.tile([P, PACK, HALF], F32, name="third", tag="first", bufs=5)
+                bank = psum.tile([P, PACK, HALF], F32, name="third", tag="bank", bufs=8)
                 for t in range(PACK):
                     wc = slice(t * P, (t + 1) * P)
                     nc.tensor.matmul_mx(
@@ -214,63 +215,71 @@ def tile_list_ski_push_features_kernel(
                         rhs=v3_q[0][:, v3_cols].bitcast(E2M1), rhs_scale=v3_q[1][:, v3_cols],
                         start=False, stop=True,
                     )
-                copy = nc.vector.tensor_copy if (shared and u == 1) else nc.scalar.copy
-                copy(out=y[:, :, cols], in_=bank[:])
-                copy(out=y_round[:, cols, :], in_=bank[:].rearrange("p t n -> p n t"))
+                nc.scalar.copy(out=y[:, :, cols], in_=bank[:])
+            all_cols = slice(c * CHUNK, (c + 1) * CHUNK)
+            nc.sync.dma_start(out=out_0.rearrange("(p t) n -> p t n", t=PACK)[:, :, all_cols], in_=y[:])
+            return y
+
+        def store_codes(c, y):
+            y_round = held("y_round%d" % c, [P, CHUNK, PACK], BF16)
+            nc.vector.tensor_copy(
+                out=y_round[:].rearrange("p (c i) t -> p c t i", i=PACK),
+                in_=y[:].rearrange("p t (c i) -> p c t i", i=PACK),
+            )
             all_cols = slice(c * CHUNK, (c + 1) * CHUNK)
             y_codes = held("y_codes%d" % c, [P, CHUNK], U32)
             nc.vector.quantize_mx(
                 out=y_codes[:].bitcast(E4M3), scales=y_plane[:, all_cols],
                 in_=y_round[:].rearrange("p n t -> p (n t)"),
             )
-            nc.sync.dma_start(out=out_0.rearrange("(p t) n -> p t n", t=PACK)[:, :, all_cols], in_=y[:])
             nc.sync.dma_start(
                 out=out_1[0].rearrange("p m t -> p (m t)").bitcast(I32)[:, all_cols], in_=y_codes[:].bitcast(I32),
             )
 
-        def h_quant(c, h):
-            return quantize("h%d" % c, h[:].rearrange("p a n t -> p (a n t)"), 2 * CHUNK)
+        def h_quant(c, h, place=None, plane_place=None):
+            return quantize("h%d" % c, h[:].rearrange("p a n t -> p (a n t)"), 2 * CHUNK, place, plane_place)
 
         def gather_pair(name, tags, words, plane, offsets, first, count, dtype):
-            return (gather(name + "_codes", tags[0], words, offsets, first, count, dtype),
-                    gather(name + "_plane", tags[1], plane, offsets, first, count, U8))
+            picked = gather(name + "_plane", tags[1], plane, offsets, first, count, U8)
+            return gather(name + "_codes", tags[0], words, offsets, first, count, dtype), picked
 
         def part(pair, i):
             cols = slice(i * CHUNK, (i + 1) * CHUNK)
             return pair[0][:, cols], pair[1][:, cols]
 
-        def f_quant(c, silu):
-            return quantize("f%d" % c, make_f(c, silu)[:], CHUNK)
+        def f_quant(c, silu, place=None):
+            return quantize("f%d" % c, make_f(c, silu, place)[:], CHUNK)
 
         v_0 = gather_pair("v_0", ("v_0_codes", "v_0_plane"), tab, tab_plane, list1, 0, CHUNK, U32)
         tanh0 = stage1(0, *part(v_0, 0), 0)
-        v_1 = gather_pair("v_1", ("slot1", "v_1_plane"), tab, tab_plane, list1, CHUNK, CHUNK, U32)
+        v_1 = gather_pair("v_1", (34304, "v_1_plane"), tab, tab_plane, list1, CHUNK, CHUNK, U32)
         tanh1 = stage1(1, *part(v_1, 0))
-        v_high = gather_pair("v_high", ("v_0_codes", "v_high_plane"), tab, tab_plane, list1, PASS, PASS, U32)
+        v_high = gather_pair("v_high", ("v_0_codes", 33792), tab, tab_plane, list1, PASS, PASS, U32)
 
-        w2_raw0 = load_weight("w2_raw0", "slot0", w2[:PASS, :])
+        tab2 = load_bytes("tab2", 17408, tab2_words[0].rearrange("p t i -> p (t i)"), T, U32)
+        w2_raw0 = load_weight("w2_raw0", 42496, w2[:PASS, :], nc.scalar)
+        tab2_plane = zeroed_plane("tab2_plane", 50688, T, nc.gpsimd)
         load_plane(tab2_plane, tab2_scales, [nc.sync] * 4)
-        tab2 = load_bytes("tab2", "small1", tab2_words[0].rearrange("p t i -> p (t i)"), T, U32)
-        w2_raw1 = load_weight("w2_raw1", "v_0_plane", w2[PASS:, :])
-        w3_raw = load_weight("w3_raw", "v_1_plane", w3)
-        tab3 = load_bytes("tab3", "slot1", tab3_words[0], T3, U16)
-        tab3_plane = zeroed_plane("tab3_plane", "tab_plane", T3, nc.gpsimd)
-        w5_plane_raw = zeroed_plane("w5_plane_raw", "tab", N, nc.gpsimd)
-        load_plane(tab3_plane, tab3_scales, [nc.sync] * 4)
+        tab3_plane = zeroed_plane("tab3_plane", 52736, T3, nc.gpsimd)
+        load_plane(tab3_plane, tab3_scales, [nc.gpsimd] * 4)
+        w2_raw1 = load_weight("w2_raw1", 25600, w2[PASS:, :])
+        w3_raw = load_weight("w3_raw", "v_0_plane", w3, nc.scalar)
+        w4_raw = load_weight("w4_raw", "v_1_plane", w4)
+        tab3 = load_bytes("tab3", 34304, tab3_words[0], T3, U16, nc.scalar)
 
         w2_round = [round_weight("w2_round0", w2_raw0), round_weight("w2_round1", w2_raw1)]
-        w4_raw = load_weight("w4_raw", "slot0", w4)
+        w5_plane_raw = zeroed_plane("w5_plane_raw", 42496, N, nc.gpsimd)
         load_plane(w5_plane_raw, w5_scales, [nc.sync] * 4)
-        w5_raw = load_bytes("w5_raw", "v_0_plane", w5_words[0].rearrange("p c i -> p (c i)"), N, U32)
+        w5_raw = load_bytes("w5_raw", 25600, w5_words[0].rearrange("p c i -> p (c i)"), N, U32)
         tanh2 = stage1(2, *part(v_high, 0))
         w3_round = round_weight("w3_round", w3_raw, 10240)
         h0_round = make_h(0, None, tanh0, False)
         h1_round = make_h(1, 5120, tanh1, True)
         v2 = gather_pair("v2", (0, 4096), tab2, tab2_plane, list2, 0, S, U32)
-        h0 = h_quant(0, h0_round)
+        h0 = h_quant(0, h0_round, 17408, 50688)
         h1 = h_quant(1, h1_round)
-        w2_q = [quantize("w2_%d" % a, w2_round[a][:], PASS) for a in range(H // PASS)]
-        h2 = h_quant(2, make_h(2, None, tanh2, False))
+        w2_q = [quantize("w2_%d" % a, w2_round[a][:], PASS, (23552, None)[a]) for a in range(H // PASS)]
+        h2 = h_quant(2, make_h(2, 19456, tanh2, False))
         w3_q = quantize("w3", w3_round[:], PASS)
         tanh3 = stage1(3, *part(v_high, 1))
         w4_round = round_weight("w4_round", w4_raw)
@@ -279,18 +288,16 @@ def tile_list_ski_push_features_kernel(
         silu2 = stage2(2, h2, part(v2, 2), w2_q, w3_q)
         h3_round = make_h(3, 13312, tanh3, True)
         v3 = gather_pair("v3", (10240, 12288), tab3, tab3_plane, list3, 0, S, U16)
-        w5_q = (deal("w5_codes", "w5_codes", w5_raw[:].bitcast(I32), N, I32), deal("w5_plane", "w5_plane", w5_plane_raw[:], N, U8))
-        w4_q = quantize("w4", w4_round[:], PASS)
-        f0 = f_quant(0, silu0)
-        h3 = h_quant(3, h3_round)
-        stage3(0, f0, v3, w4_q, w5_q, False)
+        h3 = h_quant(3, h3_round, 34304, 52736)
         silu3 = stage2(3, h3, part(v2, 3), w2_q, w3_q)
-        f1 = f_quant(1, silu1)
-        f2 = f_quant(2, silu2)
-        stage3(1, f1, v3, w4_q, w5_q, False)
-        f3 = f_quant(3, silu3)
-        stage3(2, f2, v3, w4_q, w5_q, True)
-        stage3(3, f3, v3, w4_q, w5_q, True)
+        f0_round = make_f(0, silu0, 13312)
+        w4_q = quantize("w4", w4_round[:], PASS, 15360)
+        w5_q = (deal("w5_codes", 38400, w5_raw[:].bitcast(I32), N, I32), deal("w5_plane", 36352, w5_plane_raw[:], N, U8))
+        f0 = quantize("f0", f0_round[:], CHUNK)
+        f_q = [f0, f_quant(1, silu1, "silu0"), f_quant(2, silu2, "w4_round"), f_quant(3, silu3)]
+        y = [stage3(c, f_q[c], v3, w4_q, w5_q) for c in range(4)]
+        for c in range(4):
+            store_codes(c, y[c])
 
         for q in range(4):
             queue = nc.sync if q % 2 == 0 else nc.scalar

@@ -15,14 +15,54 @@ E4M3 = mybir.dt.float8_e4m3fn_x4
 E2M1 = mybir.dt.float4_e2m1fn_x4
 ACT = mybir.ActivationFunctionType
 MULT = mybir.AluOpType.mult
-ADD = mybir.AluOpType.add
 
 P = 128
 PACK = 4
 PASS = P * PACK
+H_PASSES = H // PASS
+QUADRANTS = 4
 CHUNK = 256
+CHUNKS = S // CHUNK
 HALF = 128
+BANKS = 8
 LIST_ROWS = 16
+GAIN_RUN = 64
+
+KIB = 1024
+AT_TANH0 = 0
+AT_V2_WORDS = AT_TANH0
+AT_V2_PLANE = AT_V2_WORDS + 4 * KIB
+AT_H1 = AT_V2_PLANE + KIB
+AT_W3_ROUND = 10 * KIB
+AT_V3_WORDS = AT_W3_ROUND
+AT_V3_PLANE = AT_V3_WORDS + 2 * KIB
+AT_H3 = AT_V3_PLANE + KIB
+AT_F0 = AT_H3
+AT_W4_WORDS = AT_F0 + 2 * KIB
+AT_TAB2 = AT_H3 + 4 * KIB
+AT_WARM_OUT = AT_TAB2 + 8 * KIB - 64
+AT_H0_WORDS = AT_TAB2
+AT_H2 = AT_H0_WORDS + 2 * KIB
+AT_W2_LOW_WORDS = AT_H2 + 4 * KIB
+AT_W2_HIGH = AT_TAB2 + 8 * KIB
+AT_W5_RAW = AT_W2_HIGH
+AT_V0_WORDS = AT_W2_HIGH + 8 * KIB - 256
+AT_TAB3 = AT_V0_WORDS + KIB - 256
+AT_H3_WORDS = AT_TAB3
+AT_W5_PLANE = AT_H3_WORDS + 2 * KIB
+AT_W5_WORDS = AT_W5_PLANE + 2 * KIB
+AT_W2_LOW = AT_TAB3 + 8 * KIB
+AT_TAB2_PLANE = AT_W2_LOW + 8 * KIB
+AT_W1_RAW = AT_TAB2_PLANE - KIB
+AT_H0_PLANE = AT_TAB2_PLANE
+AT_V1_WORDS = AT_TAB2_PLANE + 2 * KIB
+AT_V1_PLANE = AT_V1_WORDS + KIB
+AT_W1_PLANE_RAW = AT_V1_PLANE - 128
+AT_V23_PLANE = AT_V1_PLANE + CHUNK
+AT_V23_WORDS = AT_V23_PLANE + 2 * CHUNK
+AT_W3_RAW = AT_V23_WORDS + 2 * KIB
+AT_W4_RAW = AT_W3_RAW + 8 * KIB
+AT_V0_PLANE = AT_W4_RAW - 128
 
 
 def tile_list_ski_push_features_kernel(
@@ -33,109 +73,118 @@ def tile_list_ski_push_features_kernel(
     nc = tc.nc
     with ExitStack() as ctx:
         keep = ctx.enter_context(tc.tile_pool(name="keep", bufs=1))
-        reuse = ctx.enter_context(tc.tile_pool(name="reuse", bufs=1))
+        shared = ctx.enter_context(tc.tile_pool(name="shared", bufs=1))
         psum = ctx.enter_context(tc.psum_pool(name="psum", bufs=1))
 
-        def held(name, shape, dtype, place=None):
+        def sbuf(name, shape, dtype, place=None):
             if isinstance(place, int):
-                return reuse.tile(shape, dtype, name=name, align_bytes=64, offset=place)
+                return shared.tile(shape, dtype, name=name, align_bytes=64, offset=place)
             return keep.tile(shape, dtype, name=name, tag=place or name, align_bytes=64)
+
+        def bank_tile(shape):
+            return psum.tile(shape, F32, name="bank", tag="bank", bufs=BANKS)
 
         def load_list(name, src):
             tile = keep.tile([P, S // LIST_ROWS], U16, name=name)
             nc.sync.dma_start(tile[:], src)
             return tile
 
-        def load_bytes(name, tag, src, width, dtype, queue=nc.sync):
-            tile = held(name, [P, width], dtype, tag)
+        def load_words(name, place, src, width, dtype, queue):
+            tile = sbuf(name, [P, width], dtype, place)
             queue.dma_start(out=tile[:].bitcast(I32), in_=src.bitcast(I32))
             return tile
 
-        def zeroed_plane(name, tag, width, engine):
-            tile = held(name, [P, width], U8, tag)
+        def zeroed_plane(name, place, width, engine):
+            tile = sbuf(name, [P, width], U8, place)
             engine.memset(tile[:].bitcast(I32), 0)
             return tile
 
         def load_plane(tile, scales, queues):
-            for q in range(4):
+            for q in range(QUADRANTS):
                 queues[q].dma_start(
                     out=tile[32 * q : 32 * q + 4, :].bitcast(I32),
                     in_=scales[0, 4 * q : 4 * q + 4, :].bitcast(I32),
                 )
 
-        def gather(name, tag, window, offsets, first, count, dtype):
-            tile = held(name, [P, count], dtype, tag)
+        def load_weight(name, place, rows, queue):
+            raw = sbuf(name, [P, PACK, PASS], F32, place)
+            queue.dma_start(out=raw[:], in_=rows.rearrange("(p j) c -> p j c", j=PACK))
+            return raw
+
+        def gather(name, place, window, offsets, first, count, dtype):
+            tile = sbuf(name, [P, count], dtype, place)
             cols = slice(first // LIST_ROWS, (first + count) // LIST_ROWS)
             nc.vector.tensor_copy(tile[:], window[:].indirect(offsets[:, cols]))
             return tile
 
-        def load_weight(name, tag, rows, queue=nc.sync):
-            raw = held(name, [P, PACK, PASS], F32, tag)
-            queue.dma_start(out=raw[:], in_=rows.rearrange("(p j) c -> p j c", j=PACK))
-            return raw
+        def gather_operand(name, places, words, plane, offsets, first, count, dtype):
+            picked_plane = gather(name + "_plane", places[1], plane, offsets, first, count, U8)
+            return gather(name + "_words", places[0], words, offsets, first, count, dtype), picked_plane
 
-        def round_weight(name, raw, place=None, on_gpsimd=False):
-            grouped = held(name, [P, PASS * PACK], BF16, place)
-            dst = grouped[:].rearrange("p (t m j) -> p m j t", t=PACK, j=PACK)
-            src = raw[:].rearrange("p j (m t) -> p m j t", t=PACK)
-            if on_gpsimd:
-                nc.gpsimd.tensor_scalar(out=dst, in0=src, scalar1=1.0, scalar2=0.0, op0=MULT, op1=ADD)
-            else:
-                nc.scalar.copy(out=dst, in_=src)
-            return grouped
+        def chunk_of(operand, i):
+            cols = slice(i * CHUNK, (i + 1) * CHUNK)
+            return operand[0][:, cols], operand[1][:, cols]
 
-        def quantize(name, grouped, width, place=None, plane_place=None):
-            codes = held(name + "_codes", [P, width], U32, place)
-            plane = held(name + "_plane", [P, width], U8, plane_place)
-            nc.vector.quantize_mx(out=codes[:].bitcast(E4M3), scales=plane[:], in_=grouped)
-            return codes, plane
+        def deal(name, place, raw, width, dtype):
+            dealt = sbuf(name, [P, width], dtype, place)
+            nc.vector.tensor_copy(
+                out=dealt[:].rearrange("p (a t i) -> p a i t", t=PACK, i=P),
+                in_=raw.rearrange("p (a i t) -> p a i t", t=PACK, i=P),
+            )
+            return dealt
 
-        w1_plane_raw = zeroed_plane("w1_plane_raw", 33536, H, nc.vector)
-        tab_plane = zeroed_plane("tab_plane", "tab_plane", T, nc.vector)
+        def round_weight(name, raw, place=None):
+            rounded = sbuf(name, [P, PASS * PACK], BF16, place)
+            nc.scalar.copy(
+                out=rounded[:].rearrange("p (t i j) -> p i j t", t=PACK, j=PACK),
+                in_=raw[:].rearrange("p j (i t) -> p i j t", t=PACK),
+            )
+            return rounded
 
+        def quantize(name, rounded, width, words_place=None, plane_place=None):
+            words = sbuf(name + "_words", [P, width], U32, words_place)
+            plane = sbuf(name + "_plane", [P, width], U8, plane_place)
+            nc.vector.quantize_mx(out=words[:].bitcast(E4M3), scales=plane[:], in_=rounded)
+            return words, plane
+
+        tab_plane = zeroed_plane("tab_plane", None, T, nc.vector)
+        w1_plane_raw = zeroed_plane("w1_plane_raw", AT_W1_PLANE_RAW, H, nc.vector)
         list1 = load_list("list1", offs)
-        w1_raw = load_bytes("w1_raw", 49664, w1_words[0], H, U16)
+        w1_raw = load_words("w1_raw", AT_W1_RAW, w1_words[0], H, U16, nc.sync)
         list2 = load_list("list2", offs2)
         list3 = load_list("list3", offs3)
-        tab = load_bytes("tab", "tab", tab_words[0].rearrange("p t i -> p (t i)"), T, U32)
+        tab = load_words("tab", None, tab_words[0].rearrange("p t i -> p (t i)"), T, U32, nc.sync)
+        load_plane(tab_plane, tab_scales, [nc.scalar] * QUADRANTS)
         load_plane(w1_plane_raw, w1_scales, [nc.gpsimd, nc.scalar, nc.scalar, nc.scalar])
-        load_plane(tab_plane, tab_scales, [nc.scalar] * 4)
 
-        warm_in = held("warm_in", [P, 32], F32, 56768)
-        warm_out = held("warm_out", [P, 32], F32, 25472)
+        warm_in = sbuf("warm_in", [P, 1], F32)
+        warm_out = sbuf("warm_out", [P, 1], F32, AT_WARM_OUT)
         nc.vector.memset(warm_in[:], 0.0)
         nc.scalar.activation(out=warm_out[:], in_=warm_in[:], func=ACT.Silu)
-        vectors = held("vectors", [P, 3, 16], F32, 56832)
-        gain1 = vectors[:, 0, 0:8].rearrange("p (a t) -> p a t", t=PACK)
+
+        vectors = sbuf("vectors", [P, 3, 16], F32, "warm_in")
+        gain1 = vectors[:, 0, 0 : H_PASSES * PACK].rearrange("p (a t) -> p a t", t=PACK)
         bias = vectors[:, 1, 0:PACK]
         gain2 = vectors[:, 2, 0:PACK]
         nc.scalar.dma_start(out=gain1, in_=g1.rearrange("(a p t) -> p a t", p=P, t=PACK))
         nc.scalar.dma_start(out=bias, in_=b.rearrange("(p t) -> p t", t=PACK))
         nc.scalar.dma_start(out=gain2, in_=g2.rearrange("(p t) -> p t", t=PACK))
 
-        def deal(name, tag, raw, width, dtype):
-            dealt = held(name, [P, width], dtype, tag)
-            nc.vector.tensor_copy(
-                out=dealt[:].rearrange("p (a t m) -> p a m t", t=PACK, m=P),
-                in_=raw.rearrange("p (a m t) -> p a m t", t=PACK, m=P),
-            )
-            return dealt
+        w1_dealt = deal("w1_dealt", None, w1_raw[:], H, U16)
+        w1_plane = deal("w1_plane", None, w1_plane_raw[:], H, U8)
 
-        w1_codes = deal("w1_codes", "w1_codes", w1_raw[:], H, U16)
-        w1_plane = deal("w1_plane", "w1_plane", w1_plane_raw[:], H, U8)
-
-        def stage1(c, v_codes, v_plane, place=None):
-            tanh = held("tanh%d" % c, [P, H // PASS, CHUNK, PACK], F32, place)
+        def stage1(c, v_words, v_plane, place=None):
+            tanh = sbuf("tanh%d" % c, [P, H_PASSES, CHUNK, PACK], F32, place)
             for u in range(CHUNK // HALF):
                 cols = slice(u * HALF, (u + 1) * HALF)
-                for a in range(H // PASS):
-                    bank = psum.tile([P, PACK, HALF], F32, name="first", tag="bank", bufs=8)
+                for a in range(H_PASSES):
+                    bank = bank_tile([P, PACK, HALF])
                     for t in range(PACK):
-                        wc = slice(a * PASS + t * P, a * PASS + (t + 1) * P)
+                        places = slice(a * PASS + t * P, a * PASS + (t + 1) * P)
                         nc.tensor.matmul_mx(
                             out=bank[:, t, :],
-                            lhsT=w1_codes[:, wc].bitcast(E2M1), lhsT_scale=w1_plane[:, wc],
-                            rhs=v_codes[:, cols].bitcast(E4M3), rhs_scale=v_plane[:, cols],
+                            lhsT=w1_dealt[:, places].bitcast(E2M1), lhsT_scale=w1_plane[:, places],
+                            rhs=v_words[:, cols].bitcast(E4M3), rhs_scale=v_plane[:, cols],
                             start=True, stop=True,
                         )
                     nc.scalar.activation(
@@ -143,37 +192,45 @@ def tile_list_ski_push_features_kernel(
                     )
             return tanh
 
-        def make_h(c, place, tanh, on_gpsimd):
-            h = held("h%d" % c, [P, H // PASS, CHUNK, PACK], BF16, place)
-            if on_gpsimd:
-                for a in range(H // PASS):
-                    nc.gpsimd.tensor_tensor(
-                        out=h[:, a, :, :], in0=tanh[:, a, :, :],
-                        in1=gain1[:, a, :].unsqueeze(1).to_broadcast([P, CHUNK, PACK]), op=MULT,
-                    )
-            else:
-                nc.vector.tensor_tensor(
-                    out=h[:], in0=tanh[:],
-                    in1=gain1.unsqueeze(2).to_broadcast([P, H // PASS, CHUNK, PACK]), op=MULT,
+        def h_on_vector(c, tanh, place=None):
+            h = sbuf("h%d" % c, [P, H_PASSES, CHUNK, PACK], BF16, place)
+            nc.vector.tensor_tensor(
+                out=h[:], in0=tanh[:],
+                in1=gain1.unsqueeze(2).to_broadcast([P, H_PASSES, CHUNK, PACK]), op=MULT,
+            )
+            return h
+
+        def h_on_gpsimd(c, tanh, gain1_run, place):
+            h = sbuf("h%d" % c, [P, H_PASSES, CHUNK, PACK], BF16, place)
+            runs = CHUNK // GAIN_RUN
+            for a in range(H_PASSES):
+                nc.gpsimd.tensor_tensor(
+                    out=h[:, a, :, :].rearrange("p (r n) t -> p r (n t)", r=runs),
+                    in0=tanh[:, a, :, :].rearrange("p (r n) t -> p r (n t)", r=runs),
+                    in1=gain1_run[:, a, :].unsqueeze(1).to_broadcast([P, runs, GAIN_RUN * PACK]), op=MULT,
                 )
             return h
 
-        def stage2(c, h_q, v2_q, w2_q, w3_q):
-            silu = held("silu%d" % c, [P, PACK, CHUNK], F32)
-            for pair in range(2):
-                bank = psum.tile([P, 2, CHUNK], F32, name="second", tag="bank", bufs=8)
+        def quantize_h(c, h, words_place=None, plane_place=None):
+            flat = h[:].rearrange("p a n t -> p (a n t)")
+            return quantize("h%d" % c, flat, H_PASSES * CHUNK, words_place, plane_place)
+
+        def stage2(c, h_mx, v2_mx, w2_mx, w3_mx):
+            silu = sbuf("silu%d" % c, [P, PACK, CHUNK], F32)
+            for pair in range(PACK // 2):
+                bank = bank_tile([P, 2, CHUNK])
                 for e in range(2):
                     t = 2 * pair + e
-                    wc = slice(t * P, (t + 1) * P)
-                    passes = [(w3_q, v2_q[0], v2_q[1])]
-                    for a in range(H // PASS):
-                        hc = slice(a * CHUNK, (a + 1) * CHUNK)
-                        passes.append((w2_q[a], h_q[0][:, hc], h_q[1][:, hc]))
-                    for i, (w_q, codes, plane) in enumerate(passes):
+                    places = slice(t * P, (t + 1) * P)
+                    passes = [(w3_mx, v2_mx[0], v2_mx[1])]
+                    for a in range(H_PASSES):
+                        cols = slice(a * CHUNK, (a + 1) * CHUNK)
+                        passes.append((w2_mx[a], h_mx[0][:, cols], h_mx[1][:, cols]))
+                    for i, (w_mx, words, plane) in enumerate(passes):
                         nc.tensor.matmul_mx(
                             out=bank[:, e, :],
-                            lhsT=w_q[0][:, wc].bitcast(E4M3), lhsT_scale=w_q[1][:, wc],
-                            rhs=codes.bitcast(E4M3), rhs_scale=plane,
+                            lhsT=w_mx[0][:, places].bitcast(E4M3), lhsT_scale=w_mx[1][:, places],
+                            rhs=words.bitcast(E4M3), rhs_scale=plane,
                             start=(i == 0), stop=(i == len(passes) - 1),
                         )
                 for e in range(2):
@@ -183,8 +240,8 @@ def tile_list_ski_push_features_kernel(
                     )
             return silu
 
-        def make_f(c, silu, place=None):
-            f = held("f%d" % c, [P, CHUNK * PACK], BF16, place)
+        def f_on_vector(c, silu, place=None):
+            f = sbuf("f%d" % c, [P, CHUNK * PACK], BF16, place)
             nc.vector.tensor_tensor(
                 out=f[:].rearrange("p (c i t) -> p c t i", i=PACK, t=PACK),
                 in0=silu[:].rearrange("p t (c i) -> p c t i", i=PACK),
@@ -192,114 +249,131 @@ def tile_list_ski_push_features_kernel(
             )
             return f
 
-        y_plane = held("y_plane", [P, S], U8)
+        def quantize_f(c, f):
+            return quantize("f%d" % c, f[:], CHUNK)
 
-        def stage3(c, f_q, v3_q, w4_q, w5_q):
-            y = held("y%d" % c, [P, PACK, CHUNK], F32)
+        y_plane = sbuf("y_plane", [P, S], U8)
+        out_rows = out_0.rearrange("(p t) n -> p t n", t=PACK)
+
+        def stage3(c, f_mx, v3_mx, w4_mx, w5_mx, round_on_scalar):
+            halves = []
+            y_round = sbuf("y_round%d" % c, [P, CHUNK, PACK], BF16)
             for u in range(CHUNK // HALF):
                 cols = slice(u * HALF, (u + 1) * HALF)
-                first = c * CHUNK + u * HALF
-                v3_cols = slice(first, first + HALF)
-                bank = psum.tile([P, PACK, HALF], F32, name="third", tag="bank", bufs=8)
+                entries = slice(c * CHUNK + u * HALF, c * CHUNK + (u + 1) * HALF)
+                bank = bank_tile([P, PACK, HALF])
                 for t in range(PACK):
-                    wc = slice(t * P, (t + 1) * P)
+                    places = slice(t * P, (t + 1) * P)
                     nc.tensor.matmul_mx(
                         out=bank[:, t, :],
-                        lhsT=w4_q[0][:, wc].bitcast(E4M3), lhsT_scale=w4_q[1][:, wc],
-                        rhs=f_q[0][:, cols].bitcast(E4M3), rhs_scale=f_q[1][:, cols],
+                        lhsT=w4_mx[0][:, places].bitcast(E4M3), lhsT_scale=w4_mx[1][:, places],
+                        rhs=f_mx[0][:, cols].bitcast(E4M3), rhs_scale=f_mx[1][:, cols],
                         start=True, stop=False,
                     )
                     nc.tensor.matmul_mx(
                         out=bank[:, t, :],
-                        lhsT=w5_q[0][:, wc].bitcast(E4M3), lhsT_scale=w5_q[1][:, wc],
-                        rhs=v3_q[0][:, v3_cols].bitcast(E2M1), rhs_scale=v3_q[1][:, v3_cols],
+                        lhsT=w5_mx[0][:, places].bitcast(E4M3), lhsT_scale=w5_mx[1][:, places],
+                        rhs=v3_mx[0][:, entries].bitcast(E2M1), rhs_scale=v3_mx[1][:, entries],
                         start=False, stop=True,
                     )
-                nc.scalar.copy(out=y[:, :, cols], in_=bank[:])
-            all_cols = slice(c * CHUNK, (c + 1) * CHUNK)
-            nc.sync.dma_start(out=out_0.rearrange("(p t) n -> p t n", t=PACK)[:, :, all_cols], in_=y[:])
-            return y
+                y = sbuf("y%d_%d" % (c, u), [P, PACK, HALF], F32)
+                nc.scalar.copy(out=y[:], in_=bank[:])
+                nc.sync.dma_start(out=out_rows[:, :, entries], in_=y[:])
+                if round_on_scalar:
+                    nc.scalar.copy(out=y_round[:, cols, :], in_=bank[:].rearrange("p t n -> p n t"))
+                halves.append(y)
+            return halves, y_round
 
-        def store_codes(c, y):
-            y_round = held("y_round%d" % c, [P, CHUNK, PACK], BF16)
-            nc.vector.tensor_copy(
-                out=y_round[:].rearrange("p (c i) t -> p c t i", i=PACK),
-                in_=y[:].rearrange("p t (c i) -> p c t i", i=PACK),
-            )
-            all_cols = slice(c * CHUNK, (c + 1) * CHUNK)
-            y_codes = held("y_codes%d" % c, [P, CHUNK], U32)
+        def round_on_vector(halves, y_round):
+            for u, y in enumerate(halves):
+                nc.vector.tensor_copy(
+                    out=y_round[:, u * HALF : (u + 1) * HALF, :].rearrange("p (c i) t -> p c t i", i=PACK),
+                    in_=y[:].rearrange("p t (c i) -> p c t i", i=PACK),
+                )
+
+        def store_words(c, y_round):
+            entries = slice(c * CHUNK, (c + 1) * CHUNK)
+            y_words = sbuf("y_words%d" % c, [P, CHUNK], U32)
             nc.vector.quantize_mx(
-                out=y_codes[:].bitcast(E4M3), scales=y_plane[:, all_cols],
+                out=y_words[:].bitcast(E4M3), scales=y_plane[:, entries],
                 in_=y_round[:].rearrange("p n t -> p (n t)"),
             )
             nc.sync.dma_start(
-                out=out_1[0].rearrange("p m t -> p (m t)").bitcast(I32)[:, all_cols], in_=y_codes[:].bitcast(I32),
+                out=out_1[0].rearrange("p m t -> p (m t)").bitcast(I32)[:, entries], in_=y_words[:].bitcast(I32),
             )
 
-        def h_quant(c, h, place=None, plane_place=None):
-            return quantize("h%d" % c, h[:].rearrange("p a n t -> p (a n t)"), 2 * CHUNK, place, plane_place)
+        v0 = gather_operand("v0", (AT_V0_WORDS, AT_V0_PLANE), tab, tab_plane, list1, 0, CHUNK, U32)
+        tanh0 = stage1(0, *chunk_of(v0, 0), AT_TANH0)
+        gain1_run = sbuf("gain1_run", [P, H_PASSES, GAIN_RUN * PACK], F32)
+        nc.scalar.copy(
+            out=gain1_run[:].rearrange("p a (n t) -> p a n t", t=PACK),
+            in_=gain1.unsqueeze(2).to_broadcast([P, H_PASSES, GAIN_RUN, PACK]),
+        )
+        v1 = gather_operand("v1", (AT_V1_WORDS, AT_V1_PLANE), tab, tab_plane, list1, CHUNK, CHUNK, U32)
+        tanh1 = stage1(1, *chunk_of(v1, 0))
+        v23 = gather_operand("v23", (AT_V23_WORDS, AT_V23_PLANE), tab, tab_plane, list1, 2 * CHUNK, 2 * CHUNK, U32)
 
-        def gather_pair(name, tags, words, plane, offsets, first, count, dtype):
-            picked = gather(name + "_plane", tags[1], plane, offsets, first, count, U8)
-            return gather(name + "_codes", tags[0], words, offsets, first, count, dtype), picked
+        tab2 = load_words("tab2", AT_TAB2, tab2_words[0].rearrange("p t i -> p (t i)"), T, U32, nc.sync)
+        w2_low_raw = load_weight("w2_low_raw", AT_W2_LOW, w2[:PASS, :], nc.scalar)
+        tab2_plane = zeroed_plane("tab2_plane", AT_TAB2_PLANE, T, nc.gpsimd)
+        load_plane(tab2_plane, tab2_scales, [nc.sync] * QUADRANTS)
+        tab3_plane = zeroed_plane("tab3_plane", "tab_plane", T3, nc.gpsimd)
+        w2_high_raw = load_weight("w2_high_raw", AT_W2_HIGH, w2[PASS:, :], nc.sync)
+        w3_raw = load_weight("w3_raw", AT_W3_RAW, w3, nc.scalar)
+        w4_raw = load_weight("w4_raw", AT_W4_RAW, w4, nc.sync)
+        tab3 = load_words("tab3", AT_TAB3, tab3_words[0], T3, U16, nc.scalar)
+        load_plane(tab3_plane, tab3_scales, [nc.sync] * QUADRANTS)
 
-        def part(pair, i):
-            cols = slice(i * CHUNK, (i + 1) * CHUNK)
-            return pair[0][:, cols], pair[1][:, cols]
+        w2_low_round = round_weight("w2_low_round", w2_low_raw)
+        w2_high_round = round_weight("w2_high_round", w2_high_raw)
+        w5_raw = load_words("w5_raw", AT_W5_RAW, w5_words[0].rearrange("p c i -> p (c i)"), N, U32, nc.sync)
+        tanh2 = stage1(2, *chunk_of(v23, 0))
+        w3_round = round_weight("w3_round", w3_raw, AT_W3_ROUND)
 
-        def f_quant(c, silu, place=None):
-            return quantize("f%d" % c, make_f(c, silu, place)[:], CHUNK)
+        h0 = h_on_vector(0, tanh0)
+        h1 = h_on_gpsimd(1, tanh1, gain1_run, AT_H1)
+        w5_plane_raw = zeroed_plane("w5_plane_raw", "tanh1", N, nc.gpsimd)
+        load_plane(w5_plane_raw, w5_scales, [nc.sync] * QUADRANTS)
+        v2 = gather_operand("v2", (AT_V2_WORDS, AT_V2_PLANE), tab2, tab2_plane, list2, 0, S, U32)
+        h0_mx = quantize_h(0, h0, AT_H0_WORDS, AT_H0_PLANE)
+        h1_mx = quantize_h(1, h1)
+        w2_mx = [
+            quantize("w2_low", w2_low_round[:], PASS, AT_W2_LOW_WORDS),
+            quantize("w2_high", w2_high_round[:], PASS),
+        ]
+        h2_mx = quantize_h(2, h_on_vector(2, tanh2, AT_H2))
+        w3_mx = quantize("w3", w3_round[:], PASS)
 
-        v_0 = gather_pair("v_0", ("v_0_codes", "v_0_plane"), tab, tab_plane, list1, 0, CHUNK, U32)
-        tanh0 = stage1(0, *part(v_0, 0), 0)
-        v_1 = gather_pair("v_1", (34304, "v_1_plane"), tab, tab_plane, list1, CHUNK, CHUNK, U32)
-        tanh1 = stage1(1, *part(v_1, 0))
-        v_high = gather_pair("v_high", ("v_0_codes", 33792), tab, tab_plane, list1, PASS, PASS, U32)
-
-        tab2 = load_bytes("tab2", 17408, tab2_words[0].rearrange("p t i -> p (t i)"), T, U32)
-        w2_raw0 = load_weight("w2_raw0", 42496, w2[:PASS, :], nc.scalar)
-        tab2_plane = zeroed_plane("tab2_plane", 50688, T, nc.gpsimd)
-        load_plane(tab2_plane, tab2_scales, [nc.sync] * 4)
-        tab3_plane = zeroed_plane("tab3_plane", 52736, T3, nc.gpsimd)
-        load_plane(tab3_plane, tab3_scales, [nc.gpsimd] * 4)
-        w2_raw1 = load_weight("w2_raw1", 25600, w2[PASS:, :])
-        w3_raw = load_weight("w3_raw", "v_0_plane", w3, nc.scalar)
-        w4_raw = load_weight("w4_raw", "v_1_plane", w4)
-        tab3 = load_bytes("tab3", 34304, tab3_words[0], T3, U16, nc.scalar)
-
-        w2_round = [round_weight("w2_round0", w2_raw0), round_weight("w2_round1", w2_raw1)]
-        w5_plane_raw = zeroed_plane("w5_plane_raw", 42496, N, nc.gpsimd)
-        load_plane(w5_plane_raw, w5_scales, [nc.sync] * 4)
-        w5_raw = load_bytes("w5_raw", 25600, w5_words[0].rearrange("p c i -> p (c i)"), N, U32)
-        tanh2 = stage1(2, *part(v_high, 0))
-        w3_round = round_weight("w3_round", w3_raw, 10240)
-        h0_round = make_h(0, None, tanh0, False)
-        h1_round = make_h(1, 5120, tanh1, True)
-        v2 = gather_pair("v2", (0, 4096), tab2, tab2_plane, list2, 0, S, U32)
-        h0 = h_quant(0, h0_round, 17408, 50688)
-        h1 = h_quant(1, h1_round)
-        w2_q = [quantize("w2_%d" % a, w2_round[a][:], PASS, (23552, None)[a]) for a in range(H // PASS)]
-        h2 = h_quant(2, make_h(2, 19456, tanh2, False))
-        w3_q = quantize("w3", w3_round[:], PASS)
-        tanh3 = stage1(3, *part(v_high, 1))
+        tanh3 = stage1(3, *chunk_of(v23, 1))
         w4_round = round_weight("w4_round", w4_raw)
-        silu0 = stage2(0, h0, part(v2, 0), w2_q, w3_q)
-        silu1 = stage2(1, h1, part(v2, 1), w2_q, w3_q)
-        silu2 = stage2(2, h2, part(v2, 2), w2_q, w3_q)
-        h3_round = make_h(3, 13312, tanh3, True)
-        v3 = gather_pair("v3", (10240, 12288), tab3, tab3_plane, list3, 0, S, U16)
-        h3 = h_quant(3, h3_round, 34304, 52736)
-        silu3 = stage2(3, h3, part(v2, 3), w2_q, w3_q)
-        f0_round = make_f(0, silu0, 13312)
-        w4_q = quantize("w4", w4_round[:], PASS, 15360)
-        w5_q = (deal("w5_codes", 38400, w5_raw[:].bitcast(I32), N, I32), deal("w5_plane", 36352, w5_plane_raw[:], N, U8))
-        f0 = quantize("f0", f0_round[:], CHUNK)
-        f_q = [f0, f_quant(1, silu1, "silu0"), f_quant(2, silu2, "w4_round"), f_quant(3, silu3)]
-        y = [stage3(c, f_q[c], v3, w4_q, w5_q) for c in range(4)]
-        for c in range(4):
-            store_codes(c, y[c])
+        silu0 = stage2(0, h0_mx, chunk_of(v2, 0), w2_mx, w3_mx)
+        silu1 = stage2(1, h1_mx, chunk_of(v2, 1), w2_mx, w3_mx)
+        silu2 = stage2(2, h2_mx, chunk_of(v2, 2), w2_mx, w3_mx)
+        h3 = h_on_gpsimd(3, tanh3, gain1_run, AT_H3)
+        v3 = gather_operand("v3", (AT_V3_WORDS, AT_V3_PLANE), tab3, tab3_plane, list3, 0, S, U16)
+        h3_mx = quantize_h(3, h3, AT_H3_WORDS, "tab_plane")
+        silu3 = stage2(3, h3_mx, chunk_of(v2, 3), w2_mx, w3_mx)
 
-        for q in range(4):
+        f0 = f_on_vector(0, silu0, AT_F0)
+        w4_mx = quantize("w4", w4_round[:], PASS, AT_W4_WORDS)
+        w5_mx = (
+            deal("w5_dealt", AT_W5_WORDS, w5_raw[:].bitcast(I32), N, I32),
+            deal("w5_plane", AT_W5_PLANE, w5_plane_raw[:], N, U8),
+        )
+        f_mx = [
+            quantize_f(0, f0),
+            quantize_f(1, f_on_vector(1, silu1, "silu0")),
+            quantize_f(2, f_on_vector(2, silu2, "w4_round")),
+            quantize_f(3, f_on_vector(3, silu3)),
+        ]
+
+        results = [stage3(c, f_mx[c], v3, w4_mx, w5_mx, c == 0) for c in range(CHUNKS)]
+        for c, (halves, y_round) in enumerate(results):
+            if c > 0:
+                round_on_vector(halves, y_round)
+            store_words(c, y_round)
+
+        for q in range(QUADRANTS):
             queue = nc.sync if q % 2 == 0 else nc.scalar
             queue.dma_start(
                 out=out_2[0, 4 * q : 4 * q + 4, :].bitcast(I32),

@@ -26,7 +26,6 @@ CHUNKS = S // CHUNK
 HALF = 128
 BANKS = 8
 LIST_ROWS = 16
-GAIN_RUN = 64
 
 KIB = 1024
 AT_TANH0 = 0
@@ -40,29 +39,27 @@ AT_H3 = AT_V3_PLANE + KIB
 AT_F0 = AT_H3
 AT_W4_WORDS = AT_F0 + 2 * KIB
 AT_TAB2 = AT_H3 + 4 * KIB
-AT_WARM_OUT = AT_TAB2 + 8 * KIB - 64
 AT_H0_WORDS = AT_TAB2
 AT_H2 = AT_H0_WORDS + 2 * KIB
 AT_W2_LOW_WORDS = AT_H2 + 4 * KIB
-AT_W2_HIGH = AT_TAB2 + 8 * KIB
-AT_W5_RAW = AT_W2_HIGH
-AT_V0_WORDS = AT_W2_HIGH + 8 * KIB - 256
-AT_TAB3 = AT_V0_WORDS + KIB - 256
+AT_VECTORS = AT_TAB2 + 8 * KIB
+AT_TAB2_PLANE = AT_VECTORS + 256
+AT_W1_RAW = AT_VECTORS - 512
+AT_H0_PLANE = AT_TAB2_PLANE
+AT_TAB3 = AT_TAB2_PLANE + 2 * KIB
+AT_V1_WORDS = AT_TAB3
 AT_H3_WORDS = AT_TAB3
 AT_W5_PLANE = AT_H3_WORDS + 2 * KIB
 AT_W5_WORDS = AT_W5_PLANE + 2 * KIB
-AT_W2_LOW = AT_TAB3 + 8 * KIB
-AT_TAB2_PLANE = AT_W2_LOW + 8 * KIB
-AT_W1_RAW = AT_TAB2_PLANE - KIB
-AT_H0_PLANE = AT_TAB2_PLANE
-AT_V1_WORDS = AT_TAB2_PLANE + 2 * KIB
-AT_V1_PLANE = AT_V1_WORDS + KIB
-AT_W1_PLANE_RAW = AT_V1_PLANE - 128
-AT_V23_PLANE = AT_V1_PLANE + CHUNK
-AT_V23_WORDS = AT_V23_PLANE + 2 * CHUNK
-AT_W3_RAW = AT_V23_WORDS + 2 * KIB
-AT_W4_RAW = AT_W3_RAW + 8 * KIB
-AT_V0_PLANE = AT_W4_RAW - 128
+AT_TAB3_PLANE = AT_TAB3 + 8 * KIB
+AT_H3_PLANE = AT_TAB3_PLANE
+AT_V23_PLANE = AT_TAB3_PLANE + 4 * KIB
+AT_W1_PLANE_RAW = AT_V23_PLANE - 256
+AT_W2_LOW = AT_V23_PLANE + 2 * CHUNK
+AT_W2_HIGH = AT_W2_LOW + 8 * KIB
+AT_W3_RAW = AT_W2_HIGH + 8 * KIB
+AT_V0_PLANE = AT_W3_RAW - 128
+AT_W5_RAW = AT_W2_HIGH
 
 
 def tile_list_ski_push_features_kernel(
@@ -100,15 +97,15 @@ def tile_list_ski_push_features_kernel(
             return tile
 
         def load_plane(tile, scales, queues):
-            for q in range(QUADRANTS):
-                queues[q].dma_start(
-                    out=tile[32 * q : 32 * q + 4, :].bitcast(I32),
-                    in_=scales[0, 4 * q : 4 * q + 4, :].bitcast(I32),
+            for quad in range(QUADRANTS):
+                queues[quad].dma_start(
+                    out=tile[32 * quad : 32 * quad + 4, :].bitcast(I32),
+                    in_=scales[0, 4 * quad : 4 * quad + 4, :].bitcast(I32),
                 )
 
         def load_weight(name, place, rows, queue):
             raw = sbuf(name, [P, PACK, PASS], F32, place)
-            queue.dma_start(out=raw[:], in_=rows.rearrange("(p j) c -> p j c", j=PACK))
+            queue.dma_start(out=raw[:], in_=rows.rearrange("(p row) col -> p row col", row=PACK))
             return raw
 
         def gather(name, place, window, offsets, first, count, dtype):
@@ -121,8 +118,8 @@ def tile_list_ski_push_features_kernel(
             picked_plane = gather(name + "_plane", places[1], plane, offsets, first, count, U8)
             return gather(name + "_words", places[0], words, offsets, first, count, dtype), picked_plane
 
-        def chunk_of(operand, i):
-            cols = slice(i * CHUNK, (i + 1) * CHUNK)
+        def chunk_of(operand, index):
+            cols = slice(index * CHUNK, (index + 1) * CHUNK)
             return operand[0][:, cols], operand[1][:, cols]
 
         def deal(name, place, raw, width, dtype):
@@ -136,8 +133,8 @@ def tile_list_ski_push_features_kernel(
         def round_weight(name, raw, place=None):
             rounded = sbuf(name, [P, PASS * PACK], BF16, place)
             nc.scalar.copy(
-                out=rounded[:].rearrange("p (t i j) -> p i j t", t=PACK, j=PACK),
-                in_=raw[:].rearrange("p j (i t) -> p i j t", t=PACK),
+                out=rounded[:].rearrange("p (t i row) -> p i row t", t=PACK, row=PACK),
+                in_=raw[:].rearrange("p row (i t) -> p i row t", t=PACK),
             )
             return rounded
 
@@ -147,31 +144,26 @@ def tile_list_ski_push_features_kernel(
             nc.vector.quantize_mx(out=words[:].bitcast(E4M3), scales=plane[:], in_=rounded)
             return words, plane
 
-        tab_plane = zeroed_plane("tab_plane", None, T, nc.vector)
         w1_plane_raw = zeroed_plane("w1_plane_raw", AT_W1_PLANE_RAW, H, nc.vector)
+        tab_plane = zeroed_plane("tab_plane", None, T, nc.vector)
         list1 = load_list("list1", offs)
         w1_raw = load_words("w1_raw", AT_W1_RAW, w1_words[0], H, U16, nc.sync)
         list2 = load_list("list2", offs2)
         list3 = load_list("list3", offs3)
-        tab = load_words("tab", None, tab_words[0].rearrange("p t i -> p (t i)"), T, U32, nc.sync)
-        load_plane(tab_plane, tab_scales, [nc.scalar] * QUADRANTS)
+        tab = load_words("tab", None, tab_words[0].rearrange("p col byte -> p (col byte)"), T, U32, nc.sync)
         load_plane(w1_plane_raw, w1_scales, [nc.gpsimd, nc.scalar, nc.scalar, nc.scalar])
+        load_plane(tab_plane, tab_scales, [nc.scalar] * QUADRANTS)
 
-        warm_in = sbuf("warm_in", [P, 1], F32)
-        warm_out = sbuf("warm_out", [P, 1], F32, AT_WARM_OUT)
-        nc.vector.memset(warm_in[:], 0.0)
-        nc.scalar.activation(out=warm_out[:], in_=warm_in[:], func=ACT.Silu)
+        w1_dealt = deal("w1_dealt", None, w1_raw[:], H, U16)
+        w1_plane = deal("w1_plane", None, w1_plane_raw[:], H, U8)
 
-        vectors = sbuf("vectors", [P, 3, 16], F32, "warm_in")
+        vectors = sbuf("vectors", [P, 3, 16], F32, AT_VECTORS)
         gain1 = vectors[:, 0, 0 : H_PASSES * PACK].rearrange("p (a t) -> p a t", t=PACK)
         bias = vectors[:, 1, 0:PACK]
         gain2 = vectors[:, 2, 0:PACK]
         nc.scalar.dma_start(out=gain1, in_=g1.rearrange("(a p t) -> p a t", p=P, t=PACK))
         nc.scalar.dma_start(out=bias, in_=b.rearrange("(p t) -> p t", t=PACK))
         nc.scalar.dma_start(out=gain2, in_=g2.rearrange("(p t) -> p t", t=PACK))
-
-        w1_dealt = deal("w1_dealt", None, w1_raw[:], H, U16)
-        w1_plane = deal("w1_plane", None, w1_plane_raw[:], H, U8)
 
         def stage1(c, v_words, v_plane, place=None):
             tanh = sbuf("tanh%d" % c, [P, H_PASSES, CHUNK, PACK], F32, place)
@@ -188,7 +180,7 @@ def tile_list_ski_push_features_kernel(
                             start=True, stop=True,
                         )
                     nc.scalar.activation(
-                        out=tanh[:, a, cols, :], in_=bank[:].rearrange("p t n -> p n t"), func=ACT.Tanh,
+                        out=tanh[:, a, cols, :], in_=bank[:].rearrange("p t j -> p j t"), func=ACT.Tanh,
                     )
             return tanh
 
@@ -200,51 +192,49 @@ def tile_list_ski_push_features_kernel(
             )
             return h
 
-        def h_on_gpsimd(c, tanh, gain1_run, place):
+        def h_on_gpsimd(c, tanh, place):
             h = sbuf("h%d" % c, [P, H_PASSES, CHUNK, PACK], BF16, place)
-            runs = CHUNK // GAIN_RUN
             for a in range(H_PASSES):
                 nc.gpsimd.tensor_tensor(
-                    out=h[:, a, :, :].rearrange("p (r n) t -> p r (n t)", r=runs),
-                    in0=tanh[:, a, :, :].rearrange("p (r n) t -> p r (n t)", r=runs),
-                    in1=gain1_run[:, a, :].unsqueeze(1).to_broadcast([P, runs, GAIN_RUN * PACK]), op=MULT,
+                    out=h[:, a, :, :], in0=tanh[:, a, :, :],
+                    in1=gain1[:, a, :].unsqueeze(1).to_broadcast([P, CHUNK, PACK]), op=MULT,
                 )
             return h
 
         def quantize_h(c, h, words_place=None, plane_place=None):
-            flat = h[:].rearrange("p a n t -> p (a n t)")
+            flat = h[:].rearrange("p a j t -> p (a j t)")
             return quantize("h%d" % c, flat, H_PASSES * CHUNK, words_place, plane_place)
 
         def stage2(c, h_mx, v2_mx, w2_mx, w3_mx):
             silu = sbuf("silu%d" % c, [P, PACK, CHUNK], F32)
             for pair in range(PACK // 2):
                 bank = bank_tile([P, 2, CHUNK])
-                for e in range(2):
-                    t = 2 * pair + e
+                for side in range(2):
+                    t = 2 * pair + side
                     places = slice(t * P, (t + 1) * P)
                     passes = [(w3_mx, v2_mx[0], v2_mx[1])]
                     for a in range(H_PASSES):
                         cols = slice(a * CHUNK, (a + 1) * CHUNK)
                         passes.append((w2_mx[a], h_mx[0][:, cols], h_mx[1][:, cols]))
-                    for i, (w_mx, words, plane) in enumerate(passes):
+                    for step, (w_mx, words, plane) in enumerate(passes):
                         nc.tensor.matmul_mx(
-                            out=bank[:, e, :],
+                            out=bank[:, side, :],
                             lhsT=w_mx[0][:, places].bitcast(E4M3), lhsT_scale=w_mx[1][:, places],
                             rhs=words.bitcast(E4M3), rhs_scale=plane,
-                            start=(i == 0), stop=(i == len(passes) - 1),
+                            start=(step == 0), stop=(step == len(passes) - 1),
                         )
-                for e in range(2):
-                    t = 2 * pair + e
+                for side in range(2):
+                    t = 2 * pair + side
                     nc.scalar.activation(
-                        out=silu[:, t, :], in_=bank[:, e, :], func=ACT.Silu, bias=bias[:, t : t + 1],
+                        out=silu[:, t, :], in_=bank[:, side, :], func=ACT.Silu, bias=bias[:, t : t + 1],
                     )
             return silu
 
         def f_on_vector(c, silu, place=None):
             f = sbuf("f%d" % c, [P, CHUNK * PACK], BF16, place)
             nc.vector.tensor_tensor(
-                out=f[:].rearrange("p (c i t) -> p c t i", i=PACK, t=PACK),
-                in0=silu[:].rearrange("p t (c i) -> p c t i", i=PACK),
+                out=f[:].rearrange("p (run j t) -> p run t j", j=PACK, t=PACK),
+                in0=silu[:].rearrange("p t (run j) -> p run t j", j=PACK),
                 in1=gain2.unsqueeze(1).unsqueeze(3).to_broadcast([P, CHUNK // PACK, PACK, PACK]), op=MULT,
             )
             return f
@@ -253,10 +243,10 @@ def tile_list_ski_push_features_kernel(
             return quantize("f%d" % c, f[:], CHUNK)
 
         y_plane = sbuf("y_plane", [P, S], U8)
-        out_rows = out_0.rearrange("(p t) n -> p t n", t=PACK)
+        out_rows = out_0.rearrange("(p t) j -> p t j", t=PACK)
 
         def stage3(c, f_mx, v3_mx, w4_mx, w5_mx, round_on_scalar):
-            halves = []
+            y = sbuf("y%d" % c, [P, PACK, CHUNK], F32)
             y_round = sbuf("y_round%d" % c, [P, CHUNK, PACK], BF16)
             for u in range(CHUNK // HALF):
                 cols = slice(u * HALF, (u + 1) * HALF)
@@ -276,62 +266,54 @@ def tile_list_ski_push_features_kernel(
                         rhs=v3_mx[0][:, entries].bitcast(E2M1), rhs_scale=v3_mx[1][:, entries],
                         start=False, stop=True,
                     )
-                y = sbuf("y%d_%d" % (c, u), [P, PACK, HALF], F32)
-                nc.scalar.copy(out=y[:], in_=bank[:])
-                nc.sync.dma_start(out=out_rows[:, :, entries], in_=y[:])
+                nc.scalar.copy(out=y[:, :, cols], in_=bank[:])
                 if round_on_scalar:
-                    nc.scalar.copy(out=y_round[:, cols, :], in_=bank[:].rearrange("p t n -> p n t"))
-                halves.append(y)
-            return halves, y_round
+                    nc.scalar.copy(out=y_round[:, cols, :], in_=bank[:].rearrange("p t j -> p j t"))
+            nc.sync.dma_start(out=out_rows[:, :, c * CHUNK : (c + 1) * CHUNK], in_=y[:])
+            return y, y_round
 
-        def round_on_vector(halves, y_round):
-            for u, y in enumerate(halves):
-                nc.vector.tensor_copy(
-                    out=y_round[:, u * HALF : (u + 1) * HALF, :].rearrange("p (c i) t -> p c t i", i=PACK),
-                    in_=y[:].rearrange("p t (c i) -> p c t i", i=PACK),
-                )
+        def round_on_vector(y, y_round):
+            nc.vector.tensor_copy(
+                out=y_round[:].rearrange("p (run j) t -> p run t j", j=PACK),
+                in_=y[:].rearrange("p t (run j) -> p run t j", j=PACK),
+            )
 
         def store_words(c, y_round):
             entries = slice(c * CHUNK, (c + 1) * CHUNK)
             y_words = sbuf("y_words%d" % c, [P, CHUNK], U32)
             nc.vector.quantize_mx(
                 out=y_words[:].bitcast(E4M3), scales=y_plane[:, entries],
-                in_=y_round[:].rearrange("p n t -> p (n t)"),
+                in_=y_round[:].rearrange("p j t -> p (j t)"),
             )
             nc.sync.dma_start(
-                out=out_1[0].rearrange("p m t -> p (m t)").bitcast(I32)[:, entries], in_=y_words[:].bitcast(I32),
+                out=out_1[0].rearrange("p j t -> p (j t)").bitcast(I32)[:, entries], in_=y_words[:].bitcast(I32),
             )
 
-        v0 = gather_operand("v0", (AT_V0_WORDS, AT_V0_PLANE), tab, tab_plane, list1, 0, CHUNK, U32)
+        v0 = gather_operand("v0", (None, AT_V0_PLANE), tab, tab_plane, list1, 0, CHUNK, U32)
         tanh0 = stage1(0, *chunk_of(v0, 0), AT_TANH0)
-        gain1_run = sbuf("gain1_run", [P, H_PASSES, GAIN_RUN * PACK], F32)
-        nc.scalar.copy(
-            out=gain1_run[:].rearrange("p a (n t) -> p a n t", t=PACK),
-            in_=gain1.unsqueeze(2).to_broadcast([P, H_PASSES, GAIN_RUN, PACK]),
-        )
-        v1 = gather_operand("v1", (AT_V1_WORDS, AT_V1_PLANE), tab, tab_plane, list1, CHUNK, CHUNK, U32)
+        v1 = gather_operand("v1", (AT_V1_WORDS, None), tab, tab_plane, list1, CHUNK, CHUNK, U32)
         tanh1 = stage1(1, *chunk_of(v1, 0))
-        v23 = gather_operand("v23", (AT_V23_WORDS, AT_V23_PLANE), tab, tab_plane, list1, 2 * CHUNK, 2 * CHUNK, U32)
+        v23 = gather_operand("v23", ("v0_words", AT_V23_PLANE), tab, tab_plane, list1, 2 * CHUNK, 2 * CHUNK, U32)
 
-        tab2 = load_words("tab2", AT_TAB2, tab2_words[0].rearrange("p t i -> p (t i)"), T, U32, nc.sync)
+        tab2 = load_words("tab2", AT_TAB2, tab2_words[0].rearrange("p col byte -> p (col byte)"), T, U32, nc.sync)
         w2_low_raw = load_weight("w2_low_raw", AT_W2_LOW, w2[:PASS, :], nc.scalar)
         tab2_plane = zeroed_plane("tab2_plane", AT_TAB2_PLANE, T, nc.gpsimd)
         load_plane(tab2_plane, tab2_scales, [nc.sync] * QUADRANTS)
-        tab3_plane = zeroed_plane("tab3_plane", "tab_plane", T3, nc.gpsimd)
+        tab3_plane = zeroed_plane("tab3_plane", AT_TAB3_PLANE, T3, nc.gpsimd)
+        load_plane(tab3_plane, tab3_scales, [nc.gpsimd] * QUADRANTS)
         w2_high_raw = load_weight("w2_high_raw", AT_W2_HIGH, w2[PASS:, :], nc.sync)
         w3_raw = load_weight("w3_raw", AT_W3_RAW, w3, nc.scalar)
-        w4_raw = load_weight("w4_raw", AT_W4_RAW, w4, nc.sync)
+        w4_raw = load_weight("w4_raw", "v1_plane", w4, nc.sync)
         tab3 = load_words("tab3", AT_TAB3, tab3_words[0], T3, U16, nc.scalar)
-        load_plane(tab3_plane, tab3_scales, [nc.sync] * QUADRANTS)
 
         w2_low_round = round_weight("w2_low_round", w2_low_raw)
         w2_high_round = round_weight("w2_high_round", w2_high_raw)
-        w5_raw = load_words("w5_raw", AT_W5_RAW, w5_words[0].rearrange("p c i -> p (c i)"), N, U32, nc.sync)
+        w5_raw = load_words("w5_raw", AT_W5_RAW, w5_words[0].rearrange("p col byte -> p (col byte)"), N, U32, nc.sync)
         tanh2 = stage1(2, *chunk_of(v23, 0))
         w3_round = round_weight("w3_round", w3_raw, AT_W3_ROUND)
 
         h0 = h_on_vector(0, tanh0)
-        h1 = h_on_gpsimd(1, tanh1, gain1_run, AT_H1)
+        h1 = h_on_gpsimd(1, tanh1, AT_H1)
         w5_plane_raw = zeroed_plane("w5_plane_raw", "tanh1", N, nc.gpsimd)
         load_plane(w5_plane_raw, w5_scales, [nc.sync] * QUADRANTS)
         v2 = gather_operand("v2", (AT_V2_WORDS, AT_V2_PLANE), tab2, tab2_plane, list2, 0, S, U32)
@@ -349,9 +331,9 @@ def tile_list_ski_push_features_kernel(
         silu0 = stage2(0, h0_mx, chunk_of(v2, 0), w2_mx, w3_mx)
         silu1 = stage2(1, h1_mx, chunk_of(v2, 1), w2_mx, w3_mx)
         silu2 = stage2(2, h2_mx, chunk_of(v2, 2), w2_mx, w3_mx)
-        h3 = h_on_gpsimd(3, tanh3, gain1_run, AT_H3)
+        h3 = h_on_gpsimd(3, tanh3, AT_H3)
         v3 = gather_operand("v3", (AT_V3_WORDS, AT_V3_PLANE), tab3, tab3_plane, list3, 0, S, U16)
-        h3_mx = quantize_h(3, h3, AT_H3_WORDS, "tab_plane")
+        h3_mx = quantize_h(3, h3, AT_H3_WORDS, AT_H3_PLANE)
         silu3 = stage2(3, h3_mx, chunk_of(v2, 3), w2_mx, w3_mx)
 
         f0 = f_on_vector(0, silu0, AT_F0)
@@ -368,14 +350,14 @@ def tile_list_ski_push_features_kernel(
         ]
 
         results = [stage3(c, f_mx[c], v3, w4_mx, w5_mx, c == 0) for c in range(CHUNKS)]
-        for c, (halves, y_round) in enumerate(results):
+        for c, (y, y_round) in enumerate(results):
             if c > 0:
-                round_on_vector(halves, y_round)
+                round_on_vector(y, y_round)
             store_words(c, y_round)
 
-        for q in range(QUADRANTS):
-            queue = nc.sync if q % 2 == 0 else nc.scalar
+        for quad in range(QUADRANTS):
+            queue = nc.sync if quad % 2 == 0 else nc.scalar
             queue.dma_start(
-                out=out_2[0, 4 * q : 4 * q + 4, :].bitcast(I32),
-                in_=y_plane[32 * q : 32 * q + 4, :].bitcast(I32),
+                out=out_2[0, 4 * quad : 4 * quad + 4, :].bitcast(I32),
+                in_=y_plane[32 * quad : 32 * quad + 4, :].bitcast(I32),
             )

from contextlib import ExitStack

import concourse.mybir as mybir

K, H, M, N, T, T3, S = 512, 1024, 512, 512, 2048, 4096, 1024
FLOPS = 2 * S * (K * H + H * M + K * M + M * N + K * N)

F32 = mybir.dt.float32
BF16 = mybir.dt.bfloat16
I32 = mybir.dt.int32
U32 = mybir.dt.uint32
U16 = mybir.dt.uint16
U8 = mybir.dt.uint8
E4M3 = mybir.dt.float8_e4m3fn_x4
E2M1 = mybir.dt.float4_e2m1fn_x4
ACT = mybir.ActivationFunctionType
MULT = mybir.AluOpType.mult

P = 128
PACK = 4
PASS = P * PACK
H_PASSES = H // PASS
QUADRANTS = 4
CHUNK = 256
CHUNKS = S // CHUNK
HALF = 128
BANKS = 8
LIST_ROWS = 16

KIB = 1024
AT_TANH0 = 0
AT_V2_WORDS = AT_TANH0
AT_V2_PLANE = AT_V2_WORDS + 4 * KIB
AT_H1 = AT_V2_PLANE + KIB
AT_W3_ROUND = 10 * KIB
AT_V3_WORDS = AT_W3_ROUND
AT_V3_PLANE = AT_V3_WORDS + 2 * KIB
AT_H3 = AT_V3_PLANE + KIB
AT_F0 = AT_H3
AT_W4_WORDS = AT_F0 + 2 * KIB
AT_TAB2 = AT_H3 + 4 * KIB
AT_H0_WORDS = AT_TAB2
AT_H2 = AT_H0_WORDS + 2 * KIB
AT_W2_LOW_WORDS = AT_H2 + 4 * KIB
AT_VECTORS = AT_TAB2 + 8 * KIB
AT_TAB2_PLANE = AT_VECTORS + 256
AT_W1_RAW = AT_VECTORS - 512
AT_H0_PLANE = AT_TAB2_PLANE
AT_TAB3 = AT_TAB2_PLANE + 2 * KIB
AT_V1_WORDS = AT_TAB3
AT_H3_WORDS = AT_TAB3
AT_W5_PLANE = AT_H3_WORDS + 2 * KIB
AT_W5_WORDS = AT_W5_PLANE + 2 * KIB
AT_TAB3_PLANE = AT_TAB3 + 8 * KIB
AT_H3_PLANE = AT_TAB3_PLANE
AT_V23_PLANE = AT_TAB3_PLANE + 4 * KIB
AT_W1_PLANE_RAW = AT_V23_PLANE - 256
AT_W2_LOW = AT_V23_PLANE + 2 * CHUNK
AT_W2_HIGH = AT_W2_LOW + 8 * KIB
AT_W3_RAW = AT_W2_HIGH + 8 * KIB
AT_V0_PLANE = AT_W3_RAW - 128
AT_W5_RAW = AT_W2_HIGH


def tile_list_ski_push_features_kernel(
    tc, tab_words, tab_scales, tab2_words, tab2_scales, tab3_words, tab3_scales,
    offs, offs2, offs3, w1_words, w1_scales, w2, w3, w4, w5_words, w5_scales, g1, b, g2,
    out_0, out_1, out_2,
):
    nc = tc.nc
    with ExitStack() as ctx:
        keep = ctx.enter_context(tc.tile_pool(name="keep", bufs=1))
        shared = ctx.enter_context(tc.tile_pool(name="shared", bufs=1))
        psum = ctx.enter_context(tc.psum_pool(name="psum", bufs=1))

        def sbuf(name, shape, dtype, place=None):
            if isinstance(place, int):
                return shared.tile(shape, dtype, name=name, align_bytes=64, offset=place)
            return keep.tile(shape, dtype, name=name, tag=place or name, align_bytes=64)

        def bank_tile(shape):
            return psum.tile(shape, F32, name="bank", tag="bank", bufs=BANKS)

        def load_list(name, src):
            tile = keep.tile([P, S // LIST_ROWS], U16, name=name)
            nc.sync.dma_start(tile[:], src)
            return tile

        def load_words(name, place, src, width, dtype, queue):
            tile = sbuf(name, [P, width], dtype, place)
            queue.dma_start(out=tile[:].bitcast(I32), in_=src.bitcast(I32))
            return tile

        def zeroed_plane(name, place, width, engine):
            tile = sbuf(name, [P, width], U8, place)
            engine.memset(tile[:].bitcast(I32), 0)
            return tile

        def load_plane(tile, scales, queues):
            for quad in range(QUADRANTS):
                queues[quad].dma_start(
                    out=tile[32 * quad : 32 * quad + 4, :].bitcast(I32),
                    in_=scales[0, 4 * quad : 4 * quad + 4, :].bitcast(I32),
                )

        def load_weight(name, place, rows, queue):
            raw = sbuf(name, [P, PACK, PASS], F32, place)
            queue.dma_start(out=raw[:], in_=rows.rearrange("(p row) col -> p row col", row=PACK))
            return raw

        def gather(name, place, window, offsets, first, count, dtype):
            tile = sbuf(name, [P, count], dtype, place)
            cols = slice(first // LIST_ROWS, (first + count) // LIST_ROWS)
            nc.vector.tensor_copy(tile[:], window[:].indirect(offsets[:, cols]))
            return tile

        def gather_operand(name, places, words, plane, offsets, first, count, dtype):
            picked_plane = gather(name + "_plane", places[1], plane, offsets, first, count, U8)
            return gather(name + "_words", places[0], words, offsets, first, count, dtype), picked_plane

        def chunk_of(operand, index):
            cols = slice(index * CHUNK, (index + 1) * CHUNK)
            return operand[0][:, cols], operand[1][:, cols]

        def deal(name, place, raw, width, dtype):
            dealt = sbuf(name, [P, width], dtype, place)
            nc.vector.tensor_copy(
                out=dealt[:].rearrange("p (a t i) -> p a i t", t=PACK, i=P),
                in_=raw.rearrange("p (a i t) -> p a i t", t=PACK, i=P),
            )
            return dealt

        def round_weight(name, raw, place=None):
            rounded = sbuf(name, [P, PASS * PACK], BF16, place)
            nc.scalar.copy(
                out=rounded[:].rearrange("p (t i row) -> p i row t", t=PACK, row=PACK),
                in_=raw[:].rearrange("p row (i t) -> p i row t", t=PACK),
            )
            return rounded

        def quantize(name, rounded, width, words_place=None, plane_place=None):
            words = sbuf(name + "_words", [P, width], U32, words_place)
            plane = sbuf(name + "_plane", [P, width], U8, plane_place)
            nc.vector.quantize_mx(out=words[:].bitcast(E4M3), scales=plane[:], in_=rounded)
            return words, plane

        w1_plane_raw = zeroed_plane("w1_plane_raw", AT_W1_PLANE_RAW, H, nc.vector)
        tab_plane = zeroed_plane("tab_plane", None, T, nc.vector)
        list1 = load_list("list1", offs)
        w1_raw = load_words("w1_raw", AT_W1_RAW, w1_words[0], H, U16, nc.sync)
        list2 = load_list("list2", offs2)
        list3 = load_list("list3", offs3)
        tab = load_words("tab", None, tab_words[0].rearrange("p col byte -> p (col byte)"), T, U32, nc.sync)
        load_plane(w1_plane_raw, w1_scales, [nc.gpsimd, nc.scalar, nc.scalar, nc.scalar])
        load_plane(tab_plane, tab_scales, [nc.scalar] * QUADRANTS)

        w1_dealt = deal("w1_dealt", None, w1_raw[:], H, U16)
        w1_plane = deal("w1_plane", None, w1_plane_raw[:], H, U8)

        vectors = sbuf("vectors", [P, 3, 16], F32, AT_VECTORS)
        gain1 = vectors[:, 0, 0 : H_PASSES * PACK].rearrange("p (a t) -> p a t", t=PACK)
        bias = vectors[:, 1, 0:PACK]
        gain2 = vectors[:, 2, 0:PACK]
        nc.scalar.dma_start(out=gain1, in_=g1.rearrange("(a p t) -> p a t", p=P, t=PACK))
        nc.scalar.dma_start(out=bias, in_=b.rearrange("(p t) -> p t", t=PACK))
        nc.scalar.dma_start(out=gain2, in_=g2.rearrange("(p t) -> p t", t=PACK))

        def stage1(c, v_words, v_plane, place=None):
            tanh = sbuf("tanh%d" % c, [P, H_PASSES, CHUNK, PACK], F32, place)
            for u in range(CHUNK // HALF):
                cols = slice(u * HALF, (u + 1) * HALF)
                for a in range(H_PASSES):
                    bank = bank_tile([P, PACK, HALF])
                    for t in range(PACK):
                        places = slice(a * PASS + t * P, a * PASS + (t + 1) * P)
                        nc.tensor.matmul_mx(
                            out=bank[:, t, :],
                            lhsT=w1_dealt[:, places].bitcast(E2M1), lhsT_scale=w1_plane[:, places],
                            rhs=v_words[:, cols].bitcast(E4M3), rhs_scale=v_plane[:, cols],
                            start=True, stop=True,
                        )
                    nc.scalar.activation(
                        out=tanh[:, a, cols, :], in_=bank[:].rearrange("p t j -> p j t"), func=ACT.Tanh,
                    )
            return tanh

        def h_on_vector(c, tanh, place=None):
            h = sbuf("h%d" % c, [P, H_PASSES, CHUNK, PACK], BF16, place)
            nc.vector.tensor_tensor(
                out=h[:], in0=tanh[:],
                in1=gain1.unsqueeze(2).to_broadcast([P, H_PASSES, CHUNK, PACK]), op=MULT,
            )
            return h

        def h_on_gpsimd(c, tanh, place):
            h = sbuf("h%d" % c, [P, H_PASSES, CHUNK, PACK], BF16, place)
            for a in range(H_PASSES):
                nc.gpsimd.tensor_tensor(
                    out=h[:, a, :, :], in0=tanh[:, a, :, :],
                    in1=gain1[:, a, :].unsqueeze(1).to_broadcast([P, CHUNK, PACK]), op=MULT,
                )
            return h

        def quantize_h(c, h, words_place=None, plane_place=None):
            flat = h[:].rearrange("p a j t -> p (a j t)")
            return quantize("h%d" % c, flat, H_PASSES * CHUNK, words_place, plane_place)

        def stage2(c, h_mx, v2_mx, w2_mx, w3_mx):
            silu = sbuf("silu%d" % c, [P, PACK, CHUNK], F32)
            for pair in range(PACK // 2):
                bank = bank_tile([P, 2, CHUNK])
                for side in range(2):
                    t = 2 * pair + side
                    places = slice(t * P, (t + 1) * P)
                    passes = [(w3_mx, v2_mx[0], v2_mx[1])]
                    for a in range(H_PASSES):
                        cols = slice(a * CHUNK, (a + 1) * CHUNK)
                        passes.append((w2_mx[a], h_mx[0][:, cols], h_mx[1][:, cols]))
                    for step, (w_mx, words, plane) in enumerate(passes):
                        nc.tensor.matmul_mx(
                            out=bank[:, side, :],
                            lhsT=w_mx[0][:, places].bitcast(E4M3), lhsT_scale=w_mx[1][:, places],
                            rhs=words.bitcast(E4M3), rhs_scale=plane,
                            start=(step == 0), stop=(step == len(passes) - 1),
                        )
                for side in range(2):
                    t = 2 * pair + side
                    nc.scalar.activation(
                        out=silu[:, t, :], in_=bank[:, side, :], func=ACT.Silu, bias=bias[:, t : t + 1],
                    )
            return silu

        def f_on_vector(c, silu, place=None):
            f = sbuf("f%d" % c, [P, CHUNK * PACK], BF16, place)
            nc.vector.tensor_tensor(
                out=f[:].rearrange("p (run j t) -> p run t j", j=PACK, t=PACK),
                in0=silu[:].rearrange("p t (run j) -> p run t j", j=PACK),
                in1=gain2.unsqueeze(1).unsqueeze(3).to_broadcast([P, CHUNK // PACK, PACK, PACK]), op=MULT,
            )
            return f

        def quantize_f(c, f):
            return quantize("f%d" % c, f[:], CHUNK)

        y_plane = sbuf("y_plane", [P, S], U8)
        out_rows = out_0.rearrange("(p t) j -> p t j", t=PACK)

        def stage3(c, f_mx, v3_mx, w4_mx, w5_mx, round_on_scalar):
            y = sbuf("y%d" % c, [P, PACK, CHUNK], F32)
            y_round = sbuf("y_round%d" % c, [P, CHUNK, PACK], BF16)
            for u in range(CHUNK // HALF):
                cols = slice(u * HALF, (u + 1) * HALF)
                entries = slice(c * CHUNK + u * HALF, c * CHUNK + (u + 1) * HALF)
                bank = bank_tile([P, PACK, HALF])
                for t in range(PACK):
                    places = slice(t * P, (t + 1) * P)
                    nc.tensor.matmul_mx(
                        out=bank[:, t, :],
                        lhsT=w4_mx[0][:, places].bitcast(E4M3), lhsT_scale=w4_mx[1][:, places],
                        rhs=f_mx[0][:, cols].bitcast(E4M3), rhs_scale=f_mx[1][:, cols],
                        start=True, stop=False,
                    )
                    nc.tensor.matmul_mx(
                        out=bank[:, t, :],
                        lhsT=w5_mx[0][:, places].bitcast(E4M3), lhsT_scale=w5_mx[1][:, places],
                        rhs=v3_mx[0][:, entries].bitcast(E2M1), rhs_scale=v3_mx[1][:, entries],
                        start=False, stop=True,
                    )
                nc.scalar.copy(out=y[:, :, cols], in_=bank[:])
                if round_on_scalar:
                    nc.scalar.copy(out=y_round[:, cols, :], in_=bank[:].rearrange("p t j -> p j t"))
            nc.sync.dma_start(out=out_rows[:, :, c * CHUNK : (c + 1) * CHUNK], in_=y[:])
            return y, y_round

        def round_on_vector(y, y_round):
            nc.vector.tensor_copy(
                out=y_round[:].rearrange("p (run j) t -> p run t j", j=PACK),
                in_=y[:].rearrange("p t (run j) -> p run t j", j=PACK),
            )

        def store_words(c, y_round):
            entries = slice(c * CHUNK, (c + 1) * CHUNK)
            y_words = sbuf("y_words%d" % c, [P, CHUNK], U32)
            nc.vector.quantize_mx(
                out=y_words[:].bitcast(E4M3), scales=y_plane[:, entries],
                in_=y_round[:].rearrange("p j t -> p (j t)"),
            )
            nc.sync.dma_start(
                out=out_1[0].rearrange("p j t -> p (j t)").bitcast(I32)[:, entries], in_=y_words[:].bitcast(I32),
            )

        v0 = gather_operand("v0", (None, AT_V0_PLANE), tab, tab_plane, list1, 0, CHUNK, U32)
        tanh0 = stage1(0, *chunk_of(v0, 0), AT_TANH0)
        v1 = gather_operand("v1", (AT_V1_WORDS, None), tab, tab_plane, list1, CHUNK, CHUNK, U32)
        tanh1 = stage1(1, *chunk_of(v1, 0))
        v23 = gather_operand("v23", ("v0_words", AT_V23_PLANE), tab, tab_plane, list1, 2 * CHUNK, 2 * CHUNK, U32)

        tab2 = load_words("tab2", AT_TAB2, tab2_words[0].rearrange("p col byte -> p (col byte)"), T, U32, nc.sync)
        w2_low_raw = load_weight("w2_low_raw", AT_W2_LOW, w2[:PASS, :], nc.scalar)
        tab2_plane = zeroed_plane("tab2_plane", AT_TAB2_PLANE, T, nc.gpsimd)
        load_plane(tab2_plane, tab2_scales, [nc.sync] * QUADRANTS)
        tab3_plane = zeroed_plane("tab3_plane", AT_TAB3_PLANE, T3, nc.gpsimd)
        load_plane(tab3_plane, tab3_scales, [nc.gpsimd] * QUADRANTS)
        w2_high_raw = load_weight("w2_high_raw", AT_W2_HIGH, w2[PASS:, :], nc.sync)
        w3_raw = load_weight("w3_raw", AT_W3_RAW, w3, nc.scalar)
        w4_raw = load_weight("w4_raw", "v1_plane", w4, nc.sync)
        tab3 = load_words("tab3", AT_TAB3, tab3_words[0], T3, U16, nc.scalar)

        w2_low_round = round_weight("w2_low_round", w2_low_raw)
        w2_high_round = round_weight("w2_high_round", w2_high_raw)
        w5_raw = load_words("w5_raw", AT_W5_RAW, w5_words[0].rearrange("p col byte -> p (col byte)"), N, U32, nc.sync)
        tanh2 = stage1(2, *chunk_of(v23, 0))
        w3_round = round_weight("w3_round", w3_raw, AT_W3_ROUND)

        h0 = h_on_vector(0, tanh0)
        h1 = h_on_gpsimd(1, tanh1, AT_H1)
        w5_plane_raw = zeroed_plane("w5_plane_raw", "tanh1", N, nc.gpsimd)
        load_plane(w5_plane_raw, w5_scales, [nc.sync] * QUADRANTS)
        v2 = gather_operand("v2", (AT_V2_WORDS, AT_V2_PLANE), tab2, tab2_plane, list2, 0, S, U32)
        h0_mx = quantize_h(0, h0, AT_H0_WORDS, AT_H0_PLANE)
        h1_mx = quantize_h(1, h1)
        w2_mx = [
            quantize("w2_low", w2_low_round[:], PASS, AT_W2_LOW_WORDS),
            quantize("w2_high", w2_high_round[:], PASS),
        ]
        h2_mx = quantize_h(2, h_on_vector(2, tanh2, AT_H2))
        w3_mx = quantize("w3", w3_round[:], PASS)

        tanh3 = stage1(3, *chunk_of(v23, 1))
        w4_round = round_weight("w4_round", w4_raw)
        silu0 = stage2(0, h0_mx, chunk_of(v2, 0), w2_mx, w3_mx)
        silu1 = stage2(1, h1_mx, chunk_of(v2, 1), w2_mx, w3_mx)
        silu2 = stage2(2, h2_mx, chunk_of(v2, 2), w2_mx, w3_mx)
        h3 = h_on_gpsimd(3, tanh3, AT_H3)
        v3 = gather_operand("v3", (AT_V3_WORDS, AT_V3_PLANE), tab3, tab3_plane, list3, 0, S, U16)
        h3_mx = quantize_h(3, h3, AT_H3_WORDS, AT_H3_PLANE)
        silu3 = stage2(3, h3_mx, chunk_of(v2, 3), w2_mx, w3_mx)

        f0 = f_on_vector(0, silu0, AT_F0)
        w4_mx = quantize("w4", w4_round[:], PASS, AT_W4_WORDS)
        w5_mx = (
            deal("w5_dealt", AT_W5_WORDS, w5_raw[:].bitcast(I32), N, I32),
            deal("w5_plane", AT_W5_PLANE, w5_plane_raw[:], N, U8),
        )
        f_mx = [
            quantize_f(0, f0),
            quantize_f(1, f_on_vector(1, silu1, "silu0")),
            quantize_f(2, f_on_vector(2, silu2, "w4_round")),
            quantize_f(3, f_on_vector(3, silu3)),
        ]

        results = [stage3(c, f_mx[c], v3, w4_mx, w5_mx, c == 0) for c in range(CHUNKS)]
        for c, (y, y_round) in enumerate(results):
            if c > 0:
                round_on_vector(y, y_round)
            store_words(c, y_round)

        for quad in range(QUADRANTS):
            queue = nc.sync if quad % 2 == 0 else nc.scalar
            queue.dma_start(
                out=out_2[0, 4 * quad : 4 * quad + 4, :].bitcast(I32),
                in_=y_plane[32 * quad : 32 * quad + 4, :].bitcast(I32),
            )
